import numpy as np
import ml_dtypes


def mxq(x, axis, fmt="e4m3"):
    dtype, down = {"e4m3": (ml_dtypes.float8_e4m3fn, 7), "e5m2": (ml_dtypes.float8_e5m2, 14)}[fmt]
    v = np.moveaxis(np.asarray(x, np.float32).astype(ml_dtypes.bfloat16).astype(np.float64), axis, -1)
    blocks = v.reshape(v.shape[:-1] + (-1, 32))
    amax = np.abs(blocks).max(-1, keepdims=True)
    byte = np.maximum(np.where(amax > 0, np.frexp(amax)[1] - 1 + 127, 0) - down, 1)
    scale = np.exp2(byte - 127.0)
    codes = (blocks / scale).astype(np.float32).astype(dtype).astype(np.float64)
    return np.moveaxis((codes * scale).reshape(v.shape), -1, axis)


WIDE = False


def mx_kscale(k):
    if not WIDE:
        return np.ones(k)
    levels = np.array([10, -10, 5, -5, 0])
    if k % 512:
        return np.exp2(np.random.permutation(np.resize(levels, k // 32))).repeat(32)
    a = np.empty((k // 512, 16))
    for p in range(k // 512):
        a[p, :8] = np.random.permutation(np.resize(levels, 8))
        for g in range(8):
            far = levels[np.abs(levels - a[p, g]) >= 10]
            a[p, g + 8] = far[np.random.randint(len(far))]
    return np.exp2(a.ravel()).repeat(32)


def f64(x):
    return np.asarray(x).astype(np.float64)


def striped(idx):
    return np.tile(idx.reshape(-1, 16).T, (8, 1)).astype(np.uint16)


def unstriped(offs):
    return offs[:16].T.reshape(-1).astype(np.int64)


E2M1 = np.array([0.0, 0.5, 1.0, 1.5, 2.0, 3.0, 4.0, 6.0, -0.0, -0.5, -1.0, -1.5, -2.0, -3.0, -4.0, -6.0])


def pack_weight(w, fmt):
    k, n = w.shape
    w = f64(np.asarray(w, np.float32).astype(ml_dtypes.bfloat16)).reshape(k // 32, 32, n)
    amax = np.abs(w).max(1)
    if fmt == "e4m3":
        byte = np.frexp(amax)[1] - 1 + 127 - 7
    else:
        mant, ex = np.frexp(amax / 6.0)
        byte = np.where(mant > 0.5, ex, ex - 1) + 127
    byte = np.clip(np.where(amax > 0, byte, 1), 1, 254)
    scaled = (w * np.exp2(127.0 - byte)[:, None, :]).reshape(k, n).astype(np.float32)
    by_word = np.ascontiguousarray(scaled.reshape(k // 512, 128, 4, n).transpose(0, 1, 3, 2))
    if fmt == "e4m3":
        words = by_word.astype(ml_dtypes.float8_e4m3fn).view(np.uint8)
    else:
        c = by_word.astype(ml_dtypes.float4_e2m1fn).view(np.uint8) & 0xF
        words = (c[..., 0::2] | (c[..., 1::2] << 4)).reshape(k // 512, 128, 2 * n)
    return np.ascontiguousarray(words), np.ascontiguousarray(byte.astype(np.uint8).reshape(k // 512, 16, n))


def unpack_weight(words, scales, fmt):
    g, _, n = scales.shape
    words = np.ascontiguousarray(words).reshape(g, 128, n, -1)
    if fmt == "e4m3":
        vals = words.view(ml_dtypes.float8_e4m3fn).astype(np.float64)
    else:
        nib = np.empty((g, 128, n, 4), np.uint8)
        nib[..., 0::2] = words & 0xF
        nib[..., 1::2] = words >> 4
        vals = E2M1[nib]
    vals = vals * np.repeat(np.exp2(scales.astype(np.float64) - 127.0), 8, axis=1)[..., None]
    return vals.transpose(0, 1, 3, 2).reshape(g * 512, n)


def gelu(v):
    return 0.5 * v * (1.0 + np.tanh(np.sqrt(2.0 / np.pi) * (v + 0.044715 * v**3)))


def bf(x):
    return np.asarray(x, np.float32).astype(ml_dtypes.bfloat16)


def planes(Y):
    n, m = Y.shape
    b = f64(bf(Y)).reshape(n // 32, 32, m)
    amax = np.abs(b).max(1)
    byte = np.clip(np.where(amax > 0, np.frexp(amax)[1] - 1 + 127 - 7, 1), 1, 254)
    codes = (b * np.exp2(127.0 - byte)[:, None, :]).reshape(n, m).astype(np.float32).astype(ml_dtypes.float8_e4m3fn).view(np.uint8)
    words = codes.reshape(n // 512, 128, 4, m).transpose(0, 1, 3, 2)
    return np.ascontiguousarray(words), np.ascontiguousarray(byte.astype(np.uint8).reshape(n // 512, 16, m))


K, T, S, P, H, N = 1536, 4096, 1024, 512, 1024, 512

def setup_inputs():
    n = np.random.standard_normal
    s = mx_kscale(K)[:, None]
    u = mx_kscale(H)[:, None]
    d = {}
    d["tab_words"], d["tab_scales"] = pack_weight(n((K, T)) * s, "e2m1")
    d["offs"] = striped(np.random.permutation(T)[:S])
    d["pos1"] = striped(np.random.permutation(S)[:P])
    d["pos2"] = striped(np.random.permutation(S)[:P])
    d["w1"] = (0.55 * n((K, H)) / s / K ** 0.5).astype(np.float32)
    d["gs"] = (2.0 * np.exp(0.3 * n(H)) * u[:, 0]).astype(np.float32)
    d["w4_words"], d["w4_scales"] = pack_weight(0.85 * n((H, H)) / u / H ** 0.5, "e2m1")
    d["ge"] = (1.2 * np.exp(0.3 * n(H)) * u[:, 0]).astype(np.float32)
    d["w3"] = (n((H, N)) / u / H ** 0.5 * np.exp(0.8 * n(N))).astype(np.float32)
    return d

def reference(tab_words, tab_scales, offs, pos1, pos2, w1, gs, w4_words, w4_scales, ge, w3):
    v = unpack_weight(tab_words, tab_scales, "e2m1")[:, unstriped(offs)]
    h = f64(gs)[:, None] * np.sin(mxq(f64(w1), 0, "e4m3").T @ v)
    cur = h[:, unstriped(pos1)]
    arc = h[:, unstriped(pos2)]
    dl = mxq(cur - arc, 0, "e4m3")
    w4 = unpack_weight(w4_words, w4_scales, "e2m1")
    e = np.tanh(w4.T @ dl)
    z = f64(ge)[:, None] * e + np.maximum(cur, arc)
    y = mxq(f64(w3), 0, "e4m3").T @ mxq(z, 0, "e4m3")
    words, scales = planes(y)
    return y, words, scales

@@ -1,0 +1,427 @@
+import math
+from contextlib import ExitStack
+
+import concourse.mybir as mybir
+
+K, T, S, PAIRS, H, N = 1536, 4096, 1024, 512, 1024, 512
+FLOPS = 2 * (K * H * S + H * H * PAIRS + H * N * PAIRS)
+
+F32 = mybir.dt.float32
+BF16 = mybir.dt.bfloat16
+I32 = mybir.dt.int32
+U32 = mybir.dt.uint32
+U16 = mybir.dt.uint16
+U8 = mybir.dt.uint8
+FP8X4 = mybir.dt.float8_e4m3fn_x4
+FP4X4 = mybir.dt.float4_e2m1fn_x4
+ACT = mybir.ActivationFunctionType
+ALU = mybir.AluOpType
+
+P = 128
+PACK = 4
+GROUP = P * PACK
+BANK = 512
+HALF = PAIRS // 2
+TWO_PI = 2.0 * math.pi
+ROUNDER = 1.5 * 2.0**23
+RR = "ABBBBBBC"
+GSV = ()
+BIGBUFS = 4
+
+
+def tile_list_tile_lot_joining_kernel(
+    tc, tab_words, tab_scales, offs, pos1, pos2, w1, gs, w4_words, w4_scales, ge, w3, out_0, out_1, out_2
+):
+    nc = tc.nc
+    with ExitStack() as ctx:
+        keep = ctx.enter_context(tc.tile_pool(name="keep", bufs=1))
+        ring = ctx.enter_context(tc.tile_pool(name="ring", bufs=2))
+        psum = ctx.enter_context(tc.psum_pool(name="psum", bufs=8))
+
+        def bank():
+            return psum.tile([P, BANK], F32, name="bank")
+
+        def big(shape, dtype):
+            return ring.tile(shape, dtype, name="big", bufs=BIGBUFS, align_bytes=64)
+
+        def load_list(src, name):
+            lst = keep.tile([P, src.shape[1]], U16, name=name)
+            nc.sync.dma_start(lst[:], src)
+            return lst
+
+        def load_rows(w, a, b):
+            raw = big([P, PACK, GROUP], F32)
+            rows = w[a * GROUP : (a + 1) * GROUP, b * GROUP : (b + 1) * GROUP]
+            nc.sync.dma_start(raw[:], rows.rearrange("(p j) c -> p j c", j=PACK))
+            return raw
+
+        def load_table(a):
+            words = big([P, T], U16)
+            nc.sync.dma_start(words[:].bitcast(I32), tab_words[a].bitcast(I32))
+            return words
+
+        def round_weight(raw, vector_share):
+            dealt = ring.tile([P, PACK * GROUP], BF16, name="dealt", bufs=3, align_bytes=64)
+            dst = dealt[:].rearrange("p (t m j) -> p m j t", t=PACK, j=PACK)
+            src = raw[:].rearrange("p j (m t) -> p m j t", t=PACK)
+            if vector_share < P:
+                nc.scalar.copy(dst[:, vector_share:], src[:, vector_share:])
+            if vector_share > 0:
+                nc.vector.tensor_copy(dst[:, :vector_share], src[:, :vector_share])
+            return dealt
+
+        def quantize(values, name):
+            width = values.shape[1] // PACK
+            codes = keep.tile([P, width], U32, name=name + "_codes", align_bytes=64)
+            scales = keep.tile([P, width], U8, name=name + "_scales", align_bytes=64)
+            nc.vector.quantize_mx(out=codes[:].bitcast(FP8X4), scales=scales[:], in_=values[:])
+            return codes, scales
+
+        def woven(flat):
+            return flat.rearrange("p (c i t) -> p c t i", i=4, t=PACK)
+
+        def planar(rows):
+            return rows.rearrange("p t (c i) -> p c t i", i=4)
+
+        offs_sb = load_list(offs, "offs_sb")
+        tab_sc = keep.tile([P, T], U8, name="tab_sc", align_bytes=64)
+        nc.vector.memset(tab_sc[:].bitcast(I32), 0)
+        w4_sc_raw = keep.tile([P, H], U8, name="w4_sc_raw", align_bytes=64)
+        nc.vector.memset(w4_sc_raw[:].bitcast(I32), 0)
+        warm = keep.tile([P, 8], F32, name="warm")
+        nc.gpsimd.memset(warm[:], 0.0)
+        nc.scalar.activation(warm[:], warm[:], ACT.Silu)
+        tab0 = load_table(0)
+        for q in range(4):
+            nc.sync.dma_start(
+                tab_sc[32 * q : 32 * q + 12, :].bitcast(I32), tab_scales[:, 4 * q : 4 * q + 4, :].bitcast(I32)
+            )
+        raw00 = load_rows(w1, 0, 0)
+        tab1 = load_table(1)
+        raw10 = load_rows(w1, 1, 0)
+        tab2 = load_table(2)
+        raw20 = load_rows(w1, 2, 0)
+
+        v_words = [keep.tile([P, S], U16, name="v_words%d" % a, align_bytes=64) for a in range(3)]
+        v_scales = [keep.tile([P, S], U8, name="v_scales%d" % a, align_bytes=64) for a in range(3)]
+        w1q = {}
+
+        nc.vector.tensor_copy(v_scales[0][:], tab_sc[:].indirect(offs_sb[:]))
+        nc.vector.tensor_copy(v_words[0][:], tab0[:].indirect(offs_sb[:]))
+        d00 = round_weight(raw00, 0)
+        for a in (1, 2):
+            nc.gpsimd.dma_start(v_scales[a][0:100, :].bitcast(I32), v_scales[0][4 * a : 4 * a + 100, :].bitcast(I32))
+        nc.vector.tensor_copy(v_words[1][:], tab1[:].indirect(offs_sb[:]))
+        d10 = round_weight(raw10, 0)
+        w1q[0, 0] = quantize(d00, "w1q00")
+        w1q[1, 0] = quantize(d10, "w1q10")
+        nc.vector.tensor_copy(v_words[2][:], tab2[:].indirect(offs_sb[:]))
+        d20 = round_weight(raw20, 80)
+        w1q[2, 0] = quantize(d20, "w1q20")
+
+        w4_raw = keep.tile([P, 2, H], U16, name="w4_raw", align_bytes=64)
+        nc.sync.dma_start(w4_raw[:].bitcast(I32), w4_words.rearrange("a p c -> p a c").bitcast(I32))
+        gs_sb = keep.tile([P, 2, PACK], F32, name="gs_sb")
+        nc.sync.dma_start(gs_sb[:], gs.rearrange("(b p t) -> p b t", p=P, t=PACK))
+        pos1_sb = load_list(pos1, "pos1_sb")
+        pos2_sb = load_list(pos2, "pos2_sb")
+        raw1 = [load_rows(w1, a, 1) for a in range(3)]
+        for q in range(4):
+            nc.sync.dma_start(
+                w4_sc_raw[32 * q : 32 * q + 8, :].bitcast(I32), w4_scales[:, 4 * q : 4 * q + 4, :].bitcast(I32)
+            )
+        ge_sb = keep.tile([P, 2, PACK], F32, name="ge_sb")
+        nc.sync.dma_start(ge_sb[:], ge.rearrange("(b p t) -> p b t", p=P, t=PACK))
+        raw3 = [load_rows(w3, a, 0) for a in range(2)]
+
+        def first_pass(acc, a, b, t, s):
+            codes, scales = w1q[a, b]
+            rows = slice(t * P, (t + 1) * P)
+            cols = slice(s * BANK, (s + 1) * BANK)
+            nc.tensor.matmul_mx(
+                out=acc[:],
+                lhsT=codes[:, rows].bitcast(FP8X4),
+                lhsT_scale=scales[:, rows],
+                rhs=v_words[a][:, cols].bitcast(FP4X4),
+                rhs_scale=v_scales[a][:, cols],
+                start=(a == 0),
+                stop=(a == 2),
+            )
+
+        acc1 = {}
+        for t in range(PACK):
+            for s in range(2):
+                acc1[0, t, s] = bank()
+        for a in range(3):
+            for t in range(PACK):
+                for s in range(2):
+                    first_pass(acc1[0, t, s], a, 0, t, s)
+
+        h = {}
+        turns_int = {}
+
+        def product(b, t):
+            for s in range(2):
+                acc1[b, t, s] = bank()
+                for a in range(3):
+                    first_pass(acc1[b, t, s], a, b, t, s)
+
+        def turns(b, t):
+            h[b, t] = keep.tile([P, S], F32, name="h%d%d" % (b, t))
+            kind = RR[4 * b + t]
+            if kind == "A":
+                return
+            if kind == "C":
+                turns_int[b, t] = ring.tile([P, S], I32, name="whole")
+            for s in range(2):
+                cols = slice(s * BANK, (s + 1) * BANK)
+                nc.scalar.activation(h[b, t][:, cols], acc1[b, t, s][:], ACT.Copy, scale=1.0 / TWO_PI)
+                if kind == "C":
+                    nc.scalar.activation(
+                        turns_int[b, t][:, cols].bitcast(U32), acc1[b, t, s][:], ACT.Copy, scale=1.0 / TWO_PI, bias=ROUNDER
+                    )
+
+        def whole_turns(b, t):
+            kind = RR[4 * b + t]
+            if kind == "C":
+                return
+            turns_int[b, t] = ring.tile([P, S], I32, name="whole")
+            if kind == "B":
+                nc.vector.tensor_copy(turns_int[b, t][:], h[b, t][:])
+            else:
+                for s in range(2):
+                    cols = slice(s * BANK, (s + 1) * BANK)
+                    nc.vector.tensor_scalar(turns_int[b, t][:, cols], acc1[b, t, s][:], 1.0 / TWO_PI, None, ALU.mult)
+
+        def fraction(b, t):
+            kind = RR[4 * b + t]
+            if kind == "B":
+                nc.vector.tensor_tensor(h[b, t][:], h[b, t][:], turns_int[b, t][:], ALU.subtract)
+            elif kind == "C":
+                nc.vector.scalar_tensor_tensor(
+                    h[b, t][:], turns_int[b, t][:], ROUNDER, h[b, t][:], ALU.subtract, ALU.subtract
+                )
+            else:
+                for s in range(2):
+                    cols = slice(s * BANK, (s + 1) * BANK)
+                    nc.vector.scalar_tensor_tensor(
+                        h[b, t][:, cols], acc1[b, t, s][:], 1.0 / TWO_PI, turns_int[b, t][:, cols], ALU.mult, ALU.subtract
+                    )
+
+        def sine(b, t):
+            sign = -1.0 if RR[4 * b + t] == "C" else 1.0
+            nc.scalar.activation(h[b, t][:], h[b, t][:], ACT.Sin, scale=sign * TWO_PI)
+            if 4 * b + t not in GSV:
+                nc.scalar.activation(h[b, t][:], h[b, t][:], ACT.Copy, scale=gs_sb[:, b, t : t + 1])
+
+        def gain(b, t):
+            if 4 * b + t in GSV:
+                nc.vector.tensor_scalar(h[b, t][:], h[b, t][:], gs_sb[:, b, t : t + 1], None, ALU.mult)
+
+        cur = {}
+        arc = {}
+        top = {}
+        for b, width in ((0, PAIRS), (1, HALF)):
+            cur[b, 0] = keep.tile([P, PACK, width], F32, name="cur%d" % b)
+            arc[b, 0] = keep.tile([P, PACK, width], F32, name="arc%d" % b)
+        cur[1, 1], arc[1, 1] = cur[1, 0], arc[1, 0]
+        top[0, 0], top[1, 1] = cur[0, 0], cur[1, 1]
+        top[1, 0] = keep.tile([P, PACK, HALF], F32, name="top10")
+
+        def pick_one(dst, lst, b, t, u):
+            k = dst[b, u].shape[2] // 16
+            nc.vector.tensor_copy(dst[b, u][:, t, :], h[b, t][:].indirect(lst[:, u * k : (u + 1) * k]))
+
+        def pick(b, t, u):
+            if u == 0:
+                gain(b, t)
+            pick_one(cur, pos1_sb, b, t, u)
+            pick_one(arc, pos2_sb, b, t, u)
+
+        dl = {}
+        dlq = {}
+
+        def difference(b, u):
+            width = cur[b, u].shape[2]
+            dl[b, u] = ring.tile([P, PACK * width], BF16, name="dl", align_bytes=64)
+            nc.vector.tensor_tensor(woven(dl[b, u][:]), planar(cur[b, u][:]), planar(arc[b, u][:]), ALU.subtract)
+
+        def larger(b, u):
+            nc.vector.tensor_tensor(top[b, u][:], cur[b, u][:], arc[b, u][:], ALU.max)
+
+        w4_dealt = keep.tile([P, 2, H], U16, name="w4_dealt", align_bytes=64)
+        w4_sc = [keep.tile([P, H], U8, name="w4_sc%d" % a, align_bytes=64) for a in range(2)]
+
+        def deal_w4_words():
+            nc.vector.tensor_copy(
+                w4_dealt[:].rearrange("p a (b t q) -> p (a b) q t", t=PACK, q=P),
+                w4_raw[:].rearrange("p a (b q t) -> p (a b) q t", t=PACK, q=P),
+            )
+
+        def deal_w4_scales():
+            nc.vector.tensor_copy(
+                w4_sc[0][:].rearrange("p (b t q) -> p b q t", t=PACK, q=P),
+                w4_sc_raw[:].rearrange("p (b q t) -> p b q t", t=PACK, q=P),
+            )
+            nc.gpsimd.dma_start(w4_sc[1][0:100, :].bitcast(I32), w4_sc[0][4:104, :].bitcast(I32))
+
+        turns(0, 0)
+        turns(0, 1)
+        deal_w4_words()
+        whole_turns(0, 0)
+        whole_turns(0, 1)
+        fraction(0, 0)
+        fraction(0, 1)
+        d01 = round_weight(raw1[0], 0)
+        turns(0, 2)
+        sine(0, 0)
+        turns(0, 3)
+        sine(0, 1)
+        whole_turns(0, 2)
+        w1q[0, 1] = quantize(d01, "w1q01")
+        fraction(0, 2)
+        whole_turns(0, 3)
+        d11 = round_weight(raw1[1], 0)
+        pick(0, 0, 0)
+        fraction(0, 3)
+        sine(0, 2)
+        d21 = round_weight(raw1[2], 0)
+        pick(0, 1, 0)
+        w1q[1, 1] = quantize(d11, "w1q11")
+        sine(0, 3)
+        deal_w4_scales()
+        w1q[2, 1] = quantize(d21, "w1q21")
+        for t in range(PACK):
+            product(1, t)
+        pick(0, 2, 0)
+        turns(1, 0)
+        turns(1, 1)
+        pick(0, 3, 0)
+
+        whole_turns(1, 0)
+        difference(0, 0)
+        fraction(1, 0)
+        turns(1, 2)
+        sine(1, 0)
+        whole_turns(1, 1)
+        dlq[0, 0] = quantize(dl[0, 0], "dlq00")
+        fraction(1, 1)
+        turns(1, 3)
+        sine(1, 1)
+        whole_turns(1, 2)
+        pick(1, 0, 0)
+        fraction(1, 2)
+        sine(1, 2)
+        whole_turns(1, 3)
+        pick(1, 1, 0)
+        fraction(1, 3)
+        sine(1, 3)
+        pick(1, 2, 0)
+        larger(0, 0)
+        pick(1, 3, 0)
+        d3 = [round_weight(raw3[a], 0) for a in range(2)]
+        difference(1, 0)
+        larger(1, 0)
+        dlq[1, 0] = quantize(dl[1, 0], "dlq10")
+
+        e = {}
+
+        def second_stage(u):
+            for b in range(2):
+                e[b, u] = ring.tile([P, PACK, HALF], F32, name="e", bufs=3)
+                for pair in range(2):
+                    acc = bank()
+                    for i in range(2):
+                        t = 2 * pair + i
+                        rows = slice((b * PACK + t) * P, (b * PACK + t + 1) * P)
+                        for q in range(2):
+                            for a in range(2):
+                                codes, scales = dlq[0, 0] if a == 0 else dlq[1, u]
+                                first = q * P + (u * HALF if a == 0 else 0)
+                                cols = slice(first, first + P)
+                                nc.tensor.matmul_mx(
+                                    out=acc[:, i * HALF + q * P : i * HALF + (q + 1) * P],
+                                    lhsT=w4_dealt[:, a, rows].bitcast(FP4X4),
+                                    lhsT_scale=w4_sc[a][:, rows],
+                                    rhs=codes[:, cols].bitcast(FP8X4),
+                                    rhs_scale=scales[:, cols],
+                                    start=(a == 0),
+                                    stop=(a == 1),
+                                )
+                    nc.scalar.activation(
+                        e[b, u][:, 2 * pair : 2 * pair + 2, :].rearrange("p t j -> p (t j)"), acc[:], ACT.Tanh
+                    )
+                    for t in (2 * pair, 2 * pair + 1):
+                        nc.scalar.activation(e[b, u][:, t, :], e[b, u][:, t, :], ACT.Copy, scale=ge_sb[:, b, t : t + 1])
+
+        z = {}
+        zq = {}
+
+        def blend(b, u):
+            z[b, u] = ring.tile([P, PACK * HALF], BF16, name="z", bufs=3, align_bytes=64)
+            best = top[0, 0][:, :, u * HALF : (u + 1) * HALF] if b == 0 else top[1, u][:]
+            nc.vector.tensor_tensor(woven(z[b, u][:]), planar(e[b, u][:]), planar(best), ALU.add)
+
+        y_codes = keep.tile([P, PAIRS], U32, name="y_codes", align_bytes=64)
+        y_scales = keep.tile([P, PAIRS], U8, name="y_scales", align_bytes=64)
+        y = {}
+        y16 = {}
+        w3q = {}
+
+        def third_stage(u):
+            y[u] = ring.tile([P, PACK, HALF], F32, name="y")
+            for pair in range(2):
+                acc = bank()
+                for i in range(2):
+                    t = 2 * pair + i
+                    rows = slice(t * P, (t + 1) * P)
+                    for a in range(2):
+                        nc.tensor.matmul_mx(
+                            out=acc[:, i * HALF : (i + 1) * HALF],
+                            lhsT=w3q[a][0][:, rows].bitcast(FP8X4),
+                            lhsT_scale=w3q[a][1][:, rows],
+                            rhs=zq[a, u][0][:].bitcast(FP8X4),
+                            rhs_scale=zq[a, u][1][:],
+                            start=(a == 0),
+                            stop=(a == 1),
+                        )
+                nc.scalar.copy(y[u][:, 2 * pair : 2 * pair + 2, :].rearrange("p t j -> p (t j)"), acc[:])
+            nc.sync.dma_start(out_0.rearrange("(p t) j -> p t j", t=PACK)[:, :, u * HALF : (u + 1) * HALF], y[u][:])
+
+        def round_result(u):
+            y16[u] = ring.tile([P, PACK * HALF], BF16, name="y16", align_bytes=64)
+            nc.vector.tensor_copy(woven(y16[u][:]), planar(y[u][:]))
+
+        def planes(u):
+            cols = slice(u * HALF, (u + 1) * HALF)
+            nc.vector.quantize_mx(out=y_codes[:, cols].bitcast(FP8X4), scales=y_scales[:, cols], in_=y16[u][:])
+            nc.sync.dma_start(
+                out_1[0].rearrange("p m t -> p (m t)").bitcast(I32)[:, cols], y_codes[:, cols].bitcast(I32)
+            )
+
+        second_stage(0)
+        for t in range(PACK):
+            pick(1, t, 1)
+        difference(1, 1)
+        w3q[0] = quantize(d3[0], "w3q0")
+        dlq[1, 1] = quantize(dl[1, 1], "dlq11")
+        second_stage(1)
+        blend(0, 0)
+        w3q[1] = quantize(d3[1], "w3q1")
+        blend(1, 0)
+        zq[0, 0] = quantize(z[0, 0], "zq00")
+        larger(1, 1)
+        zq[1, 0] = quantize(z[1, 0], "zq10")
+        third_stage(0)
+        blend(0, 1)
+        blend(1, 1)
+        zq[0, 1] = quantize(z[0, 1], "zq01")
+        zq[1, 1] = quantize(z[1, 1], "zq11")
+        third_stage(1)
+        round_result(0)
+        planes(0)
+        round_result(1)
+        planes(1)
+        for q in range(4):
+            queue = nc.sync if q % 2 == 0 else nc.scalar
+            queue.dma_start(out_2[0, 4 * q : 4 * q + 4, :].bitcast(I32), y_scales[32 * q : 32 * q + 4, :].bitcast(I32))

@@ -24,9 +24,14 @@ BANK = 512
 HALF = PAIRS // 2
 TWO_PI = 2.0 * math.pi
 ROUNDER = 1.5 * 2.0**23
-RR = "ABBBBBBC"
+RR = "ABBBCCCC"
 GSV = ()
 BIGBUFS = 4
+CHUNKS = [256, 256]
+STARTS = [sum(CHUNKS[:u]) for u in range(len(CHUNKS))]
+RUN = 2
+Y16S = (0,)
+GEV = ()
 
 
 def tile_list_tile_lot_joining_kernel(
@@ -60,8 +65,9 @@ def tile_list_tile_lot_joining_kernel(
             nc.sync.dma_start(words[:].bitcast(I32), tab_words[a].bitcast(I32))
             return words
 
-        def round_weight(raw, vector_share):
-            dealt = ring.tile([P, PACK * GROUP], BF16, name="dealt", bufs=3, align_bytes=64)
+        def round_weight(raw, vector_share, dealt=None):
+            if dealt is None:
+                dealt = ring.tile([P, PACK * GROUP], BF16, name="dealt", bufs=3, align_bytes=64)
             dst = dealt[:].rearrange("p (t m j) -> p m j t", t=PACK, j=PACK)
             src = raw[:].rearrange("p j (m t) -> p m j t", t=PACK)
             if vector_share < P:
@@ -77,11 +83,11 @@ def tile_list_tile_lot_joining_kernel(
             nc.vector.quantize_mx(out=codes[:].bitcast(FP8X4), scales=scales[:], in_=values[:])
             return codes, scales
 
-        def woven(flat):
-            return flat.rearrange("p (c i t) -> p c t i", i=4, t=PACK)
+        def woven(flat, run):
+            return flat.rearrange("p (c i t) -> p c t i", i=run, t=PACK)
 
-        def planar(rows):
-            return rows.rearrange("p t (c i) -> p c t i", i=4)
+        def planar(rows, run):
+            return rows.rearrange("p t (c i) -> p c t i", i=run)
 
         offs_sb = load_list(offs, "offs_sb")
         tab_sc = keep.tile([P, T], U8, name="tab_sc", align_bytes=64)
@@ -92,11 +98,11 @@ def tile_list_tile_lot_joining_kernel(
         nc.gpsimd.memset(warm[:], 0.0)
         nc.scalar.activation(warm[:], warm[:], ACT.Silu)
         tab0 = load_table(0)
+        raw00 = load_rows(w1, 0, 0)
         for q in range(4):
             nc.sync.dma_start(
                 tab_sc[32 * q : 32 * q + 12, :].bitcast(I32), tab_scales[:, 4 * q : 4 * q + 4, :].bitcast(I32)
             )
-        raw00 = load_rows(w1, 0, 0)
         tab1 = load_table(1)
         raw10 = load_rows(w1, 1, 0)
         tab2 = load_table(2)
@@ -106,11 +112,11 @@ def tile_list_tile_lot_joining_kernel(
         v_scales = [keep.tile([P, S], U8, name="v_scales%d" % a, align_bytes=64) for a in range(3)]
         w1q = {}
 
-        nc.vector.tensor_copy(v_scales[0][:], tab_sc[:].indirect(offs_sb[:]))
         nc.vector.tensor_copy(v_words[0][:], tab0[:].indirect(offs_sb[:]))
+        nc.vector.tensor_copy(v_scales[0][:], tab_sc[:].indirect(offs_sb[:]))
         d00 = round_weight(raw00, 0)
         for a in (1, 2):
-            nc.gpsimd.dma_start(v_scales[a][0:100, :].bitcast(I32), v_scales[0][4 * a : 4 * a + 100, :].bitcast(I32))
+            nc.scalar.dma_start(v_scales[a][0:100, :].bitcast(I32), v_scales[0][4 * a : 4 * a + 100, :].bitcast(I32))
         nc.vector.tensor_copy(v_words[1][:], tab1[:].indirect(offs_sb[:]))
         d10 = round_weight(raw10, 0)
         w1q[0, 0] = quantize(d00, "w1q00")
@@ -119,7 +125,7 @@ def tile_list_tile_lot_joining_kernel(
         d20 = round_weight(raw20, 80)
         w1q[2, 0] = quantize(d20, "w1q20")
 
-        w4_raw = keep.tile([P, 2, H], U16, name="w4_raw", align_bytes=64)
+        w4_raw = big([P, 2, H], U16)
         nc.sync.dma_start(w4_raw[:].bitcast(I32), w4_words.rearrange("a p c -> p a c").bitcast(I32))
         gs_sb = keep.tile([P, 2, PACK], F32, name="gs_sb")
         nc.sync.dma_start(gs_sb[:], gs.rearrange("(b p t) -> p b t", p=P, t=PACK))
@@ -172,7 +178,7 @@ def tile_list_tile_lot_joining_kernel(
             if kind == "A":
                 return
             if kind == "C":
-                turns_int[b, t] = ring.tile([P, S], I32, name="whole")
+                turns_int[b, t] = ring.tile([P, S], I32, name="whole", bufs=3, align_bytes=64)
             for s in range(2):
                 cols = slice(s * BANK, (s + 1) * BANK)
                 nc.scalar.activation(h[b, t][:, cols], acc1[b, t, s][:], ACT.Copy, scale=1.0 / TWO_PI)
@@ -185,7 +191,7 @@ def tile_list_tile_lot_joining_kernel(
             kind = RR[4 * b + t]
             if kind == "C":
                 return
-            turns_int[b, t] = ring.tile([P, S], I32, name="whole")
+            turns_int[b, t] = ring.tile([P, S], I32, name="whole", bufs=3, align_bytes=64)
             if kind == "B":
                 nc.vector.tensor_copy(turns_int[b, t][:], h[b, t][:])
             else:
@@ -218,36 +224,43 @@ def tile_list_tile_lot_joining_kernel(
             if 4 * b + t in GSV:
                 nc.vector.tensor_scalar(h[b, t][:], h[b, t][:], gs_sb[:, b, t : t + 1], None, ALU.mult)
 
+        last = len(CHUNKS) - 1
         cur = {}
         arc = {}
         top = {}
-        for b, width in ((0, PAIRS), (1, HALF)):
-            cur[b, 0] = keep.tile([P, PACK, width], F32, name="cur%d" % b)
-            arc[b, 0] = keep.tile([P, PACK, width], F32, name="arc%d" % b)
-        cur[1, 1], arc[1, 1] = cur[1, 0], arc[1, 0]
-        top[0, 0], top[1, 1] = cur[0, 0], cur[1, 1]
-        top[1, 0] = keep.tile([P, PACK, HALF], F32, name="top10")
-
-        def pick_one(dst, lst, b, t, u):
-            k = dst[b, u].shape[2] // 16
-            nc.vector.tensor_copy(dst[b, u][:, t, :], h[b, t][:].indirect(lst[:, u * k : (u + 1) * k]))
+        cur[0, 0] = keep.tile([P, PACK, PAIRS], F32, name="cur0")[:]
+        arc[0, 0] = keep.tile([P, PACK, PAIRS], F32, name="arc0")[:]
+        top[0, 0] = cur[0, 0]
+        cur1 = keep.tile([P, PACK * max(CHUNKS)], F32, name="cur1")
+        arc1 = keep.tile([P, PACK * max(CHUNKS)], F32, name="arc1")
+        for u, width in enumerate(CHUNKS):
+            cur[1, u] = cur1[:, : PACK * width].rearrange("p (t j) -> p t j", t=PACK)
+            arc[1, u] = arc1[:, : PACK * width].rearrange("p (t j) -> p t j", t=PACK)
+            top[1, u] = cur[1, u] if u == last else keep.tile([P, PACK, width], F32, name="top%d" % u)[:]
 
         def pick(b, t, u):
             if u == 0:
                 gain(b, t)
-            pick_one(cur, pos1_sb, b, t, u)
-            pick_one(arc, pos2_sb, b, t, u)
+            first = STARTS[u] // 16
+            part = slice(first, first + cur[b, u].shape[2] // 16)
+            nc.vector.tensor_copy(cur[b, u][:, t, :], h[b, t][:].indirect(pos1_sb[:, part]))
+            nc.vector.tensor_copy(arc[b, u][:, t, :], h[b, t][:].indirect(pos2_sb[:, part]))
 
+        w3_dealt = keep.tile([P, 2 * PACK * GROUP], BF16, name="w3_dealt", align_bytes=64)
+        d3 = {}
         dl = {}
         dlq = {}
 
         def difference(b, u):
             width = cur[b, u].shape[2]
-            dl[b, u] = ring.tile([P, PACK * width], BF16, name="dl", align_bytes=64)
-            nc.vector.tensor_tensor(woven(dl[b, u][:]), planar(cur[b, u][:]), planar(arc[b, u][:]), ALU.subtract)
+            if (b, u) == (1, 0):
+                dl[b, u] = w3_dealt[:, PACK * GROUP - 2 * width : PACK * GROUP + 2 * width]
+            else:
+                dl[b, u] = ring.tile([P, PACK * width], BF16, name="dl", align_bytes=64)
+            nc.vector.tensor_tensor(woven(dl[b, u][:], RUN), planar(cur[b, u], RUN), planar(arc[b, u], RUN), ALU.subtract)
 
         def larger(b, u):
-            nc.vector.tensor_tensor(top[b, u][:], cur[b, u][:], arc[b, u][:], ALU.max)
+            nc.vector.tensor_tensor(top[b, u], cur[b, u], arc[b, u], ALU.max)
 
         w4_dealt = keep.tile([P, 2, H], U16, name="w4_dealt", align_bytes=64)
         w4_sc = [keep.tile([P, H], U8, name="w4_sc%d" % a, align_bytes=64) for a in range(2)]
@@ -263,7 +276,7 @@ def tile_list_tile_lot_joining_kernel(
                 w4_sc[0][:].rearrange("p (b t q) -> p b q t", t=PACK, q=P),
                 w4_sc_raw[:].rearrange("p (b q t) -> p b q t", t=PACK, q=P),
             )
-            nc.gpsimd.dma_start(w4_sc[1][0:100, :].bitcast(I32), w4_sc[0][4:104, :].bitcast(I32))
+            nc.scalar.dma_start(w4_sc[1][0:100, :].bitcast(I32), w4_sc[0][4:104, :].bitcast(I32))
 
         turns(0, 0)
         turns(0, 1)
@@ -319,28 +332,26 @@ def tile_list_tile_lot_joining_kernel(
         pick(1, 2, 0)
         larger(0, 0)
         pick(1, 3, 0)
-        d3 = [round_weight(raw3[a], 0) for a in range(2)]
-        difference(1, 0)
-        larger(1, 0)
-        dlq[1, 0] = quantize(dl[1, 0], "dlq10")
 
         e = {}
 
         def second_stage(u):
+            width = CHUNKS[u]
+            share = BANK // width
             for b in range(2):
-                e[b, u] = ring.tile([P, PACK, HALF], F32, name="e", bufs=3)
-                for pair in range(2):
+                e[b, u] = ring.tile([P, PACK, width], F32, name="e", bufs=4)
+                for t0 in range(0, PACK, share):
                     acc = bank()
-                    for i in range(2):
-                        t = 2 * pair + i
+                    for i in range(share):
+                        t = t0 + i
                         rows = slice((b * PACK + t) * P, (b * PACK + t + 1) * P)
-                        for q in range(2):
+                        for q in range(0, width, P):
                             for a in range(2):
                                 codes, scales = dlq[0, 0] if a == 0 else dlq[1, u]
-                                first = q * P + (u * HALF if a == 0 else 0)
+                                first = q + (STARTS[u] if a == 0 else 0)
                                 cols = slice(first, first + P)
                                 nc.tensor.matmul_mx(
-                                    out=acc[:, i * HALF + q * P : i * HALF + (q + 1) * P],
+                                    out=acc[:, i * width + q : i * width + q + P],
                                     lhsT=w4_dealt[:, a, rows].bitcast(FP4X4),
                                     lhsT_scale=w4_sc[a][:, rows],
                                     rhs=codes[:, cols].bitcast(FP8X4),
@@ -349,18 +360,25 @@ def tile_list_tile_lot_joining_kernel(
                                     stop=(a == 1),
                                 )
                     nc.scalar.activation(
-                        e[b, u][:, 2 * pair : 2 * pair + 2, :].rearrange("p t j -> p (t j)"), acc[:], ACT.Tanh
+                        e[b, u][:, t0 : t0 + share, :].rearrange("p t j -> p (t j)"), acc[:], ACT.Tanh
                     )
-                    for t in (2 * pair, 2 * pair + 1):
-                        nc.scalar.activation(e[b, u][:, t, :], e[b, u][:, t, :], ACT.Copy, scale=ge_sb[:, b, t : t + 1])
+                    if u not in GEV:
+                        for t in range(t0, t0 + share):
+                            nc.scalar.activation(
+                                e[b, u][:, t, :], e[b, u][:, t, :], ACT.Copy, scale=ge_sb[:, b, t : t + 1]
+                            )
 
         z = {}
         zq = {}
 
         def blend(b, u):
-            z[b, u] = ring.tile([P, PACK * HALF], BF16, name="z", bufs=3, align_bytes=64)
-            best = top[0, 0][:, :, u * HALF : (u + 1) * HALF] if b == 0 else top[1, u][:]
-            nc.vector.tensor_tensor(woven(z[b, u][:]), planar(e[b, u][:]), planar(best), ALU.add)
+            width = CHUNKS[u]
+            z[b, u] = ring.tile([P, PACK * width], BF16, name="z", bufs=3, align_bytes=64)
+            best = top[0, 0][:, :, STARTS[u] : STARTS[u] + width] if b == 0 else top[1, u]
+            if u in GEV:
+                gains = ge_sb[:, b, :].unsqueeze(2).to_broadcast([P, PACK, width])
+                nc.vector.tensor_tensor(e[b, u][:], e[b, u][:], gains, ALU.mult)
+            nc.vector.tensor_tensor(woven(z[b, u][:], RUN), planar(e[b, u][:], RUN), planar(best, RUN), ALU.add)
 
         y_codes = keep.tile([P, PAIRS], U32, name="y_codes", align_bytes=64)
         y_scales = keep.tile([P, PAIRS], U8, name="y_scales", align_bytes=64)
@@ -369,15 +387,16 @@ def tile_list_tile_lot_joining_kernel(
         w3q = {}
 
         def third_stage(u):
-            y[u] = ring.tile([P, PACK, HALF], F32, name="y")
-            for pair in range(2):
+            width = CHUNKS[u]
+            share = BANK // width
+            y[u] = ring.tile([P, PACK, width], F32, name="y")
+            for t0 in range(0, PACK, share):
                 acc = bank()
-                for i in range(2):
-                    t = 2 * pair + i
-                    rows = slice(t * P, (t + 1) * P)
+                for i in range(share):
+                    rows = slice((t0 + i) * P, (t0 + i + 1) * P)
                     for a in range(2):
                         nc.tensor.matmul_mx(
-                            out=acc[:, i * HALF : (i + 1) * HALF],
+                            out=acc[:, i * width : (i + 1) * width],
                             lhsT=w3q[a][0][:, rows].bitcast(FP8X4),
                             lhsT_scale=w3q[a][1][:, rows],
                             rhs=zq[a, u][0][:].bitcast(FP8X4),
@@ -385,43 +404,52 @@ def tile_list_tile_lot_joining_kernel(
                             start=(a == 0),
                             stop=(a == 1),
                         )
-                nc.scalar.copy(y[u][:, 2 * pair : 2 * pair + 2, :].rearrange("p t j -> p (t j)"), acc[:])
-            nc.sync.dma_start(out_0.rearrange("(p t) j -> p t j", t=PACK)[:, :, u * HALF : (u + 1) * HALF], y[u][:])
+                nc.scalar.copy(y[u][:, t0 : t0 + share, :].rearrange("p t j -> p (t j)"), acc[:])
+            nc.sync.dma_start(out_0.rearrange("(p t) j -> p t j", t=PACK)[:, :, STARTS[u] : STARTS[u] + width], y[u][:])
 
         def round_result(u):
-            y16[u] = ring.tile([P, PACK * HALF], BF16, name="y16", align_bytes=64)
-            nc.vector.tensor_copy(woven(y16[u][:]), planar(y[u][:]))
+            y16[u] = ring.tile([P, PACK * CHUNKS[u]], BF16, name="y16", align_bytes=64)
+            if u in Y16S:
+                nc.scalar.copy(woven(y16[u][:], 4), planar(y[u][:], 4))
+            else:
+                nc.vector.tensor_copy(woven(y16[u][:], 4), planar(y[u][:], 4))
 
         def planes(u):
-            cols = slice(u * HALF, (u + 1) * HALF)
+            cols = slice(STARTS[u], STARTS[u] + CHUNKS[u])
             nc.vector.quantize_mx(out=y_codes[:, cols].bitcast(FP8X4), scales=y_scales[:, cols], in_=y16[u][:])
             nc.sync.dma_start(
                 out_1[0].rearrange("p m t -> p (m t)").bitcast(I32)[:, cols], y_codes[:, cols].bitcast(I32)
             )
 
-        second_stage(0)
-        for t in range(PACK):
-            pick(1, t, 1)
-        difference(1, 1)
-        w3q[0] = quantize(d3[0], "w3q0")
-        dlq[1, 1] = quantize(dl[1, 1], "dlq11")
-        second_stage(1)
-        blend(0, 0)
-        w3q[1] = quantize(d3[1], "w3q1")
-        blend(1, 0)
-        zq[0, 0] = quantize(z[0, 0], "zq00")
-        larger(1, 1)
-        zq[1, 0] = quantize(z[1, 0], "zq10")
-        third_stage(0)
-        blend(0, 1)
-        blend(1, 1)
-        zq[0, 1] = quantize(z[0, 1], "zq01")
-        zq[1, 1] = quantize(z[1, 1], "zq11")
-        third_stage(1)
-        round_result(0)
-        planes(0)
-        round_result(1)
-        planes(1)
+        for u in range(last + 3):
+            if 1 <= u <= last:
+                for t in range(PACK):
+                    pick(1, t, u)
+            if u <= last:
+                difference(1, u)
+                if u < last:
+                    larger(1, u)
+                if u == 1:
+                    w3q[0] = quantize(d3[0], "w3q0")
+                dlq[1, u] = quantize(dl[1, u], "dlq1%d" % u)
+                if u == 0:
+                    d3[0] = round_weight(raw3[0], 0, w3_dealt[:, : PACK * GROUP])
+                second_stage(u)
+                if u == 0:
+                    d3[1] = round_weight(raw3[1], 0, w3_dealt[:, PACK * GROUP :])
+                if u == 1:
+                    w3q[1] = quantize(d3[1], "w3q1")
+                if u == last:
+                    larger(1, u)
+            if 1 <= u <= last + 1:
+                blend(0, u - 1)
+                blend(1, u - 1)
+                zq[0, u - 1] = quantize(z[0, u - 1], "zq0%d" % u)
+                zq[1, u - 1] = quantize(z[1, u - 1], "zq1%d" % u)
+                third_stage(u - 1)
+            if u >= 2:
+                round_result(u - 2)
+                planes(u - 2)
         for q in range(4):
             queue = nc.sync if q % 2 == 0 else nc.scalar
             queue.dma_start(out_2[0, 4 * q : 4 * q + 4, :].bitcast(I32), y_scales[32 * q : 32 * q + 4, :].bitcast(I32))

@@ -18,8 +18,8 @@ ACT = mybir.ActivationFunctionType
 ALU = mybir.AluOpType
 
 P = 128
-PACK = 4
-GROUP = P * PACK
+PA1 = 4
+GROUP = P * PA1
 BANK = 512
 HALF = PAIRS // 2
 TWO_PI = 2.0 * math.pi
@@ -55,9 +55,9 @@ def tile_list_tile_lot_joining_kernel(
             return lst
 
         def load_rows(w, a, b):
-            raw = big([P, PACK, GROUP], F32)
+            raw = big([P, PA1, GROUP], F32)
             rows = w[a * GROUP : (a + 1) * GROUP, b * GROUP : (b + 1) * GROUP]
-            nc.sync.dma_start(raw[:], rows.rearrange("(p j) c -> p j c", j=PACK))
+            nc.sync.dma_start(raw[:], rows.rearrange("(p j) c -> p j c", j=PA1))
             return raw
 
         def load_table(a):
@@ -67,9 +67,9 @@ def tile_list_tile_lot_joining_kernel(
 
         def round_weight(raw, vector_share, dealt=None):
             if dealt is None:
-                dealt = ring.tile([P, PACK * GROUP], BF16, name="dealt", bufs=3, align_bytes=64)
-            dst = dealt[:].rearrange("p (t m j) -> p m j t", t=PACK, j=PACK)
-            src = raw[:].rearrange("p j (m t) -> p m j t", t=PACK)
+                dealt = ring.tile([P, PA1 * GROUP], BF16, name="dealt", bufs=3, align_bytes=64)
+            dst = dealt[:].rearrange("p (t m j) -> p m t j", t=PA1, j=PA1)
+            src = raw[:].rearrange("p j (m t) -> p m t j", t=PA1)
             if vector_share < P:
                 nc.scalar.copy(dst[:, vector_share:], src[:, vector_share:])
             if vector_share > 0:
@@ -77,19 +77,21 @@ def tile_list_tile_lot_joining_kernel(
             return dealt
 
         def quantize(values, name):
-            width = values.shape[1] // PACK
+            width = values.shape[1] // PA1
             codes = keep.tile([P, width], U32, name=name + "_codes", align_bytes=64)
             scales = keep.tile([P, width], U8, name=name + "_scales", align_bytes=64)
             nc.vector.quantize_mx(out=codes[:].bitcast(FP8X4), scales=scales[:], in_=values[:])
             return codes, scales
 
         def woven(flat, run):
-            return flat.rearrange("p (c i t) -> p c t i", i=run, t=PACK)
+            return flat.rearrange("p (c i t) -> p c t i", i=run, t=PA1)
 
         def planar(rows, run):
             return rows.rearrange("p t (c i) -> p c t i", i=run)
 
         offs_sb = load_list(offs, "offs_sb")
+        gs_sb = keep.tile([P, 2, PA1], F32, name="gs_sb")
+        nc.sync.dma_start(gs_sb[:], gs.rearrange("(b p t) -> p b t", p=P, t=PA1))
         tab_sc = keep.tile([P, T], U8, name="tab_sc", align_bytes=64)
         nc.vector.memset(tab_sc[:].bitcast(I32), 0)
         w4_sc_raw = keep.tile([P, H], U8, name="w4_sc_raw", align_bytes=64)
@@ -108,6 +110,10 @@ def tile_list_tile_lot_joining_kernel(
         tab2 = load_table(2)
         raw20 = load_rows(w1, 2, 0)
 
+        gs_wide = []
+        for b, width in enumerate((PAIRS, max(CHUNKS))):
+            gs_wide.append(keep.tile([P, PA1, width], F32, name="gs_wide%d" % b))
+            nc.scalar.copy(gs_wide[b][:], gs_sb[:, b, :].unsqueeze(2).to_broadcast([P, PA1, width]))
         v_words = [keep.tile([P, S], U16, name="v_words%d" % a, align_bytes=64) for a in range(3)]
         v_scales = [keep.tile([P, S], U8, name="v_scales%d" % a, align_bytes=64) for a in range(3)]
         w1q = {}
@@ -127,8 +133,6 @@ def tile_list_tile_lot_joining_kernel(
 
         w4_raw = big([P, 2, H], U16)
         nc.sync.dma_start(w4_raw[:].bitcast(I32), w4_words.rearrange("a p c -> p a c").bitcast(I32))
-        gs_sb = keep.tile([P, 2, PACK], F32, name="gs_sb")
-        nc.sync.dma_start(gs_sb[:], gs.rearrange("(b p t) -> p b t", p=P, t=PACK))
         pos1_sb = load_list(pos1, "pos1_sb")
         pos2_sb = load_list(pos2, "pos2_sb")
         raw1 = [load_rows(w1, a, 1) for a in range(3)]
@@ -136,8 +140,8 @@ def tile_list_tile_lot_joining_kernel(
             nc.sync.dma_start(
                 w4_sc_raw[32 * q : 32 * q + 8, :].bitcast(I32), w4_scales[:, 4 * q : 4 * q + 4, :].bitcast(I32)
             )
-        ge_sb = keep.tile([P, 2, PACK], F32, name="ge_sb")
-        nc.sync.dma_start(ge_sb[:], ge.rearrange("(b p t) -> p b t", p=P, t=PACK))
+        ge_sb = keep.tile([P, 2, PA1], F32, name="ge_sb")
+        nc.sync.dma_start(ge_sb[:], ge.rearrange("(b p t) -> p b t", p=P, t=PA1))
         raw3 = [load_rows(w3, a, 0) for a in range(2)]
 
         def first_pass(acc, a, b, t, s):
@@ -155,13 +159,23 @@ def tile_list_tile_lot_joining_kernel(
             )
 
         acc1 = {}
-        for t in range(PACK):
+        for t in range(PA1):
             for s in range(2):
                 acc1[0, t, s] = bank()
-        for a in range(3):
-            for t in range(PACK):
+        for t in range(PA1):
+            for s in range(2):
+                first_pass(acc1[0, t, s], 0, 0, t, s)
+        for t in range(PA1):
+            for a in (1, 2):
                 for s in range(2):
                     first_pass(acc1[0, t, s], a, 0, t, s)
+
+        w3_dealt = keep.tile([P, 2 * PA1 * GROUP], BF16, name="w3_dealt", align_bytes=64)
+
+        def whole_tile(b, t):
+            if (b, t) == (1, 3):
+                return w3_dealt[:, S : 3 * S].bitcast(I32)
+            return ring.tile([P, S], I32, name="whole", bufs=3, align_bytes=64)
 
         h = {}
         turns_int = {}
@@ -178,7 +192,7 @@ def tile_list_tile_lot_joining_kernel(
             if kind == "A":
                 return
             if kind == "C":
-                turns_int[b, t] = ring.tile([P, S], I32, name="whole", bufs=3, align_bytes=64)
+                turns_int[b, t] = whole_tile(b, t)
             for s in range(2):
                 cols = slice(s * BANK, (s + 1) * BANK)
                 nc.scalar.activation(h[b, t][:, cols], acc1[b, t, s][:], ACT.Copy, scale=1.0 / TWO_PI)
@@ -191,7 +205,7 @@ def tile_list_tile_lot_joining_kernel(
             kind = RR[4 * b + t]
             if kind == "C":
                 return
-            turns_int[b, t] = ring.tile([P, S], I32, name="whole", bufs=3, align_bytes=64)
+            turns_int[b, t] = whole_tile(b, t)
             if kind == "B":
                 nc.vector.tensor_copy(turns_int[b, t][:], h[b, t][:])
             else:
@@ -217,121 +231,90 @@ def tile_list_tile_lot_joining_kernel(
         def sine(b, t):
             sign = -1.0 if RR[4 * b + t] == "C" else 1.0
             nc.scalar.activation(h[b, t][:], h[b, t][:], ACT.Sin, scale=sign * TWO_PI)
-            if 4 * b + t not in GSV:
-                nc.scalar.activation(h[b, t][:], h[b, t][:], ACT.Copy, scale=gs_sb[:, b, t : t + 1])
-
-        def gain(b, t):
-            if 4 * b + t in GSV:
-                nc.vector.tensor_scalar(h[b, t][:], h[b, t][:], gs_sb[:, b, t : t + 1], None, ALU.mult)
 
         last = len(CHUNKS) - 1
         cur = {}
         arc = {}
         top = {}
-        cur[0, 0] = keep.tile([P, PACK, PAIRS], F32, name="cur0")[:]
-        arc[0, 0] = keep.tile([P, PACK, PAIRS], F32, name="arc0")[:]
-        top[0, 0] = cur[0, 0]
-        cur1 = keep.tile([P, PACK * max(CHUNKS)], F32, name="cur1")
-        arc1 = keep.tile([P, PACK * max(CHUNKS)], F32, name="arc1")
+        cur[0, 0] = keep.tile([P, PA1, PAIRS], F32, name="cur0")[:]
+        arc[0, 0] = keep.tile([P, PA1, PAIRS], F32, name="arc0")[:]
+        cur1 = keep.tile([P, PA1 * max(CHUNKS)], F32, name="cur1")
+        arc1 = keep.tile([P, PA1 * max(CHUNKS)], F32, name="arc1")
         for u, width in enumerate(CHUNKS):
-            cur[1, u] = cur1[:, : PACK * width].rearrange("p (t j) -> p t j", t=PACK)
-            arc[1, u] = arc1[:, : PACK * width].rearrange("p (t j) -> p t j", t=PACK)
-            top[1, u] = cur[1, u] if u == last else keep.tile([P, PACK, width], F32, name="top%d" % u)[:]
+            cur[1, u] = cur1[:, : PA1 * width].rearrange("p (t j) -> p t j", t=PA1)
+            arc[1, u] = arc1[:, : PA1 * width].rearrange("p (t j) -> p t j", t=PA1)
+            top[1, u] = cur[1, u] if u == last else keep.tile([P, PA1, width], F32, name="top%d" % u)[:]
 
         def pick(b, t, u):
-            if u == 0:
-                gain(b, t)
             first = STARTS[u] // 16
             part = slice(first, first + cur[b, u].shape[2] // 16)
-            nc.vector.tensor_copy(cur[b, u][:, t, :], h[b, t][:].indirect(pos1_sb[:, part]))
-            nc.vector.tensor_copy(arc[b, u][:, t, :], h[b, t][:].indirect(pos2_sb[:, part]))
+            gains = gs_wide[b][:, t, : cur[b, u].shape[2]]
+            nc.vector.tensor_tensor(cur[b, u][:, t, :], h[b, t][:].indirect(pos1_sb[:, part]), gains, ALU.mult)
+            nc.vector.tensor_tensor(arc[b, u][:, t, :], h[b, t][:].indirect(pos2_sb[:, part]), gains, ALU.mult)
 
-        w3_dealt = keep.tile([P, 2 * PACK * GROUP], BF16, name="w3_dealt", align_bytes=64)
         d3 = {}
         dl = {}
         dlq = {}
 
         def difference(b, u):
             width = cur[b, u].shape[2]
-            if (b, u) == (1, 0):
-                dl[b, u] = w3_dealt[:, PACK * GROUP - 2 * width : PACK * GROUP + 2 * width]
-            else:
-                dl[b, u] = ring.tile([P, PACK * width], BF16, name="dl", align_bytes=64)
+            dl[b, u] = ring.tile([P, PA1 * width], BF16, name="dl", align_bytes=64)
             nc.vector.tensor_tensor(woven(dl[b, u][:], RUN), planar(cur[b, u], RUN), planar(arc[b, u], RUN), ALU.subtract)
 
         def larger(b, u):
             nc.vector.tensor_tensor(top[b, u], cur[b, u], arc[b, u], ALU.max)
 
+        def larger_first(u):
+            cols = slice(STARTS[u], STARTS[u] + CHUNKS[u])
+            nc.vector.tensor_tensor(top[0, u], cur[0, 0][:, :, cols], arc[0, 0][:, :, cols], ALU.max)
+
         w4_dealt = keep.tile([P, 2, H], U16, name="w4_dealt", align_bytes=64)
         w4_sc = [keep.tile([P, H], U8, name="w4_sc%d" % a, align_bytes=64) for a in range(2)]
 
-        def deal_w4_words():
+        def deal_w4_words(a):
             nc.vector.tensor_copy(
-                w4_dealt[:].rearrange("p a (b t q) -> p (a b) q t", t=PACK, q=P),
-                w4_raw[:].rearrange("p a (b q t) -> p (a b) q t", t=PACK, q=P),
+                w4_dealt[:, a, :].rearrange("p (b t q) -> p b t q", t=PA1, q=P),
+                w4_raw[:, a, :].rearrange("p (b q t) -> p b t q", t=PA1, q=P),
             )
 
         def deal_w4_scales():
             nc.vector.tensor_copy(
-                w4_sc[0][:].rearrange("p (b t q) -> p b q t", t=PACK, q=P),
-                w4_sc_raw[:].rearrange("p (b q t) -> p b q t", t=PACK, q=P),
+                w4_sc[0][:].rearrange("p (b t q) -> p b t q", t=PA1, q=P),
+                w4_sc_raw[:].rearrange("p (b q t) -> p b t q", t=PA1, q=P),
             )
             nc.scalar.dma_start(w4_sc[1][0:100, :].bitcast(I32), w4_sc[0][4:104, :].bitcast(I32))
 
-        turns(0, 0)
-        turns(0, 1)
-        deal_w4_words()
-        whole_turns(0, 0)
-        whole_turns(0, 1)
-        fraction(0, 0)
-        fraction(0, 1)
-        d01 = round_weight(raw1[0], 0)
-        turns(0, 2)
-        sine(0, 0)
-        turns(0, 3)
-        sine(0, 1)
-        whole_turns(0, 2)
-        w1q[0, 1] = quantize(d01, "w1q01")
-        fraction(0, 2)
-        whole_turns(0, 3)
-        d11 = round_weight(raw1[1], 0)
-        pick(0, 0, 0)
-        fraction(0, 3)
-        sine(0, 2)
-        d21 = round_weight(raw1[2], 0)
-        pick(0, 1, 0)
-        w1q[1, 1] = quantize(d11, "w1q11")
-        sine(0, 3)
-        deal_w4_scales()
-        w1q[2, 1] = quantize(d21, "w1q21")
-        for t in range(PACK):
-            product(1, t)
-        pick(0, 2, 0)
-        turns(1, 0)
-        turns(1, 1)
-        pick(0, 3, 0)
+        tiles = [(b, t) for b in range(2) for t in range(PA1)]
+        d1 = {}
+        for k in range(len(tiles) + 2):
+            if 1 <= k <= len(tiles):
+                sine(*tiles[k - 1])
+            if 1 + 1 <= k <= 1 + 3:
+                w1q[k - 1 - 1, 1] = quantize(d1[k - 1 - 1], "w1q%d1" % (k - 1 - 1))
+            if False and 1 <= k <= 1 + 2:
+                d1[k - 1] = round_weight(raw1[k - 1], 0)
+            if k < len(tiles):
+                if k >= PA1:
+                    product(*tiles[k])
+                turns(*tiles[k])
+            if not False and 1 <= k <= 1 + 2:
+                d1[k - 1] = round_weight(raw1[k - 1], 0)
+            if k < len(tiles):
+                whole_turns(*tiles[k])
+                fraction(*tiles[k])
+            if k >= 2:
+                pick(*tiles[k - 2], 0)
+            if k < 2:
+                deal_w4_words(k)
+            if k == 2:
+                deal_w4_scales()
+            if k == 5:
+                difference(0, 0)
+            if k == 6:
+                dlq[0, 0] = quantize(dl[0, 0], "dlq00")
 
-        whole_turns(1, 0)
-        difference(0, 0)
-        fraction(1, 0)
-        turns(1, 2)
-        sine(1, 0)
-        whole_turns(1, 1)
-        dlq[0, 0] = quantize(dl[0, 0], "dlq00")
-        fraction(1, 1)
-        turns(1, 3)
-        sine(1, 1)
-        whole_turns(1, 2)
-        pick(1, 0, 0)
-        fraction(1, 2)
-        sine(1, 2)
-        whole_turns(1, 3)
-        pick(1, 1, 0)
-        fraction(1, 3)
-        sine(1, 3)
-        pick(1, 2, 0)
-        larger(0, 0)
-        pick(1, 3, 0)
+        for a in range(2):
+            d3[a] = round_weight(raw3[a], 0, w3_dealt[:, a * PA1 * GROUP : (a + 1) * PA1 * GROUP])
 
         e = {}
 
@@ -339,12 +322,12 @@ def tile_list_tile_lot_joining_kernel(
             width = CHUNKS[u]
             share = BANK // width
             for b in range(2):
-                e[b, u] = ring.tile([P, PACK, width], F32, name="e", bufs=4)
-                for t0 in range(0, PACK, share):
+                e[b, u] = ring.tile([P, PA1, width], F32, name="e", bufs=4)
+                for t0 in range(0, PA1, share):
                     acc = bank()
                     for i in range(share):
                         t = t0 + i
-                        rows = slice((b * PACK + t) * P, (b * PACK + t + 1) * P)
+                        rows = slice((b * PA1 + t) * P, (b * PA1 + t + 1) * P)
                         for q in range(0, width, P):
                             for a in range(2):
                                 codes, scales = dlq[0, 0] if a == 0 else dlq[1, u]
@@ -373,10 +356,10 @@ def tile_list_tile_lot_joining_kernel(
 
         def blend(b, u):
             width = CHUNKS[u]
-            z[b, u] = ring.tile([P, PACK * width], BF16, name="z", bufs=3, align_bytes=64)
-            best = top[0, 0][:, :, STARTS[u] : STARTS[u] + width] if b == 0 else top[1, u]
+            z[b, u] = ring.tile([P, PA1 * width], BF16, name="z", bufs=3, align_bytes=64)
+            best = top[b, u]
             if u in GEV:
-                gains = ge_sb[:, b, :].unsqueeze(2).to_broadcast([P, PACK, width])
+                gains = ge_sb[:, b, :].unsqueeze(2).to_broadcast([P, PA1, width])
                 nc.vector.tensor_tensor(e[b, u][:], e[b, u][:], gains, ALU.mult)
             nc.vector.tensor_tensor(woven(z[b, u][:], RUN), planar(e[b, u][:], RUN), planar(best, RUN), ALU.add)
 
@@ -389,8 +372,8 @@ def tile_list_tile_lot_joining_kernel(
         def third_stage(u):
             width = CHUNKS[u]
             share = BANK // width
-            y[u] = ring.tile([P, PACK, width], F32, name="y")
-            for t0 in range(0, PACK, share):
+            y[u] = ring.tile([P, PA1, width], F32, name="y")
+            for t0 in range(0, PA1, share):
                 acc = bank()
                 for i in range(share):
                     rows = slice((t0 + i) * P, (t0 + i + 1) * P)
@@ -405,10 +388,10 @@ def tile_list_tile_lot_joining_kernel(
                             stop=(a == 1),
                         )
                 nc.scalar.copy(y[u][:, t0 : t0 + share, :].rearrange("p t j -> p (t j)"), acc[:])
-            nc.sync.dma_start(out_0.rearrange("(p t) j -> p t j", t=PACK)[:, :, STARTS[u] : STARTS[u] + width], y[u][:])
+            nc.sync.dma_start(out_0.rearrange("(p t) j -> p t j", t=PA1)[:, :, STARTS[u] : STARTS[u] + width], y[u][:])
 
         def round_result(u):
-            y16[u] = ring.tile([P, PACK * CHUNKS[u]], BF16, name="y16", align_bytes=64)
+            y16[u] = ring.tile([P, PA1 * CHUNKS[u]], BF16, name="y16", align_bytes=64)
             if u in Y16S:
                 nc.scalar.copy(woven(y16[u][:], 4), planar(y[u][:], 4))
             else:
@@ -423,7 +406,7 @@ def tile_list_tile_lot_joining_kernel(
 
         for u in range(last + 3):
             if 1 <= u <= last:
-                for t in range(PACK):
+                for t in range(PA1):
                     pick(1, t, u)
             if u <= last:
                 difference(1, u)
@@ -432,11 +415,9 @@ def tile_list_tile_lot_joining_kernel(
                 if u == 1:
                     w3q[0] = quantize(d3[0], "w3q0")
                 dlq[1, u] = quantize(dl[1, u], "dlq1%d" % u)
-                if u == 0:
-                    d3[0] = round_weight(raw3[0], 0, w3_dealt[:, : PACK * GROUP])
                 second_stage(u)
-                if u == 0:
-                    d3[1] = round_weight(raw3[1], 0, w3_dealt[:, PACK * GROUP :])
+                top[0, u] = cur[0, 0][:, :, STARTS[u] : STARTS[u] + CHUNKS[u]]
+                larger_first(u)
                 if u == 1:
                     w3q[1] = quantize(d3[1], "w3q1")
                 if u == last:

@@ -18,20 +18,20 @@ ACT = mybir.ActivationFunctionType
 ALU = mybir.AluOpType
 
 P = 128
-PA1 = 4
-GROUP = P * PA1
+PACK = 4
+GROUP = P * PACK
 BANK = 512
 HALF = PAIRS // 2
+K_PASSES = K // GROUP
+H_GROUPS = H // GROUP
+QUADRANTS = 4
+SCALE_SPAN = 100
 TWO_PI = 2.0 * math.pi
 ROUNDER = 1.5 * 2.0**23
-RR = "ABBBCCCC"
-GSV = ()
-BIGBUFS = 4
-CHUNKS = [256, 256]
-STARTS = [sum(CHUNKS[:u]) for u in range(len(CHUNKS))]
-RUN = 2
-Y16S = (0,)
-GEV = ()
+
+VECTOR_ONLY_SLICES = 2
+VECTOR_SHARE = 80
+PIECES = {0: [(0, HALF)], 1: [(0, P), (P, P)]}
 
 
 def tile_list_tile_lot_joining_kernel(
@@ -46,391 +46,347 @@ def tile_list_tile_lot_joining_kernel(
         def bank():
             return psum.tile([P, BANK], F32, name="bank")
 
-        def big(shape, dtype):
-            return ring.tile(shape, dtype, name="big", bufs=BIGBUFS, align_bytes=64)
+        def streamed(shape, dtype):
+            return ring.tile(shape, dtype, name="streamed", bufs=4, align_bytes=64)
 
         def load_list(src, name):
-            lst = keep.tile([P, src.shape[1]], U16, name=name)
-            nc.sync.dma_start(lst[:], src)
-            return lst
+            offsets = keep.tile([P, src.shape[1]], U16, name=name)
+            nc.sync.dma_start(offsets[:], src)
+            return offsets
 
-        def load_rows(w, a, b):
-            raw = big([P, PA1, GROUP], F32)
-            rows = w[a * GROUP : (a + 1) * GROUP, b * GROUP : (b + 1) * GROUP]
-            nc.sync.dma_start(raw[:], rows.rearrange("(p j) c -> p j c", j=PA1))
+        def load_gain(src, name):
+            gain = keep.tile([P, H_GROUPS, PACK], F32, name=name)
+            nc.sync.dma_start(gain[:], src.rearrange("(g p t) -> p g t", p=P, t=PACK))
+            return gain
+
+        def load_weight(raw, w, a, g):
+            block = w[a * GROUP : (a + 1) * GROUP, g * GROUP : (g + 1) * GROUP]
+            nc.sync.dma_start(raw[:], block.rearrange("(p j) c -> p j c", j=PACK))
             return raw
 
-        def load_table(a):
-            words = big([P, T], U16)
+        def load_table(words, a):
             nc.sync.dma_start(words[:].bitcast(I32), tab_words[a].bitcast(I32))
             return words
 
-        def round_weight(raw, vector_share, dealt=None):
+        def load_scale_rows(rows, src):
+            live = 4 * src.shape[0]
+            for q in range(QUADRANTS):
+                nc.sync.dma_start(rows[32 * q : 32 * q + live, :].bitcast(I32), src[:, 4 * q : 4 * q + 4, :].bitcast(I32))
+
+        def lift_scale_rows(dst, packed, a):
+            nc.sync.dma_start(dst[0:SCALE_SPAN, :].bitcast(I32), packed[4 * a : 4 * a + SCALE_SPAN, :].bitcast(I32))
+
+        def round_weight(raw, vector_share=0, dealt=None):
             if dealt is None:
-                dealt = ring.tile([P, PA1 * GROUP], BF16, name="dealt", bufs=3, align_bytes=64)
-            dst = dealt[:].rearrange("p (t m j) -> p m t j", t=PA1, j=PA1)
-            src = raw[:].rearrange("p j (m t) -> p m t j", t=PA1)
-            if vector_share < P:
-                nc.scalar.copy(dst[:, vector_share:], src[:, vector_share:])
-            if vector_share > 0:
+                dealt = ring.tile([P, PACK * GROUP], BF16, name="dealt", bufs=3, align_bytes=64)
+            dst = dealt[:].rearrange("p (t m j) -> p m t j", t=PACK, j=PACK)
+            src = raw[:].rearrange("p j (m t) -> p m t j", t=PACK)
+            nc.scalar.copy(dst[:, vector_share:], src[:, vector_share:])
+            if vector_share:
                 nc.vector.tensor_copy(dst[:, :vector_share], src[:, :vector_share])
             return dealt
 
         def quantize(values, name):
-            width = values.shape[1] // PA1
+            width = values.shape[1] // PACK
             codes = keep.tile([P, width], U32, name=name + "_codes", align_bytes=64)
             scales = keep.tile([P, width], U8, name=name + "_scales", align_bytes=64)
             nc.vector.quantize_mx(out=codes[:].bitcast(FP8X4), scales=scales[:], in_=values[:])
             return codes, scales
 
         def woven(flat, run):
-            return flat.rearrange("p (c i t) -> p c t i", i=run, t=PA1)
+            return flat.rearrange("p (c i t) -> p c t i", i=run, t=PACK)
 
         def planar(rows, run):
             return rows.rearrange("p t (c i) -> p c t i", i=run)
 
         offs_sb = load_list(offs, "offs_sb")
-        gs_sb = keep.tile([P, 2, PA1], F32, name="gs_sb")
-        nc.sync.dma_start(gs_sb[:], gs.rearrange("(b p t) -> p b t", p=P, t=PA1))
+        gs_sb = load_gain(gs, "gs_sb")
+        pos1_sb = load_list(pos1, "pos1_sb")
+        pos2_sb = load_list(pos2, "pos2_sb")
+        ge_sb = load_gain(ge, "ge_sb")
         tab_sc = keep.tile([P, T], U8, name="tab_sc", align_bytes=64)
         nc.vector.memset(tab_sc[:].bitcast(I32), 0)
         w4_sc_raw = keep.tile([P, H], U8, name="w4_sc_raw", align_bytes=64)
         nc.vector.memset(w4_sc_raw[:].bitcast(I32), 0)
         warm = keep.tile([P, 8], F32, name="warm")
-        nc.gpsimd.memset(warm[:], 0.0)
+        nc.vector.memset(warm[:], 0.0)
         nc.scalar.activation(warm[:], warm[:], ACT.Silu)
-        tab0 = load_table(0)
-        raw00 = load_rows(w1, 0, 0)
-        for q in range(4):
-            nc.sync.dma_start(
-                tab_sc[32 * q : 32 * q + 12, :].bitcast(I32), tab_scales[:, 4 * q : 4 * q + 4, :].bitcast(I32)
-            )
-        tab1 = load_table(1)
-        raw10 = load_rows(w1, 1, 0)
-        tab2 = load_table(2)
-        raw20 = load_rows(w1, 2, 0)
+        w4_raw = keep.tile([P, H_GROUPS, H], U16, name="w4_raw", align_bytes=64)
+        nc.sync.dma_start(w4_raw[:].bitcast(I32), w4_words.rearrange("a p c -> p a c").bitcast(I32))
+        table = {0: load_table(keep.tile([P, T], U16, name="cur_first", align_bytes=64), 0)}
+        load_scale_rows(tab_sc, tab_scales)
+        w1_raw = {(0, 0): load_weight(keep.tile([P, PACK, GROUP], F32, name="arc_first", align_bytes=64), w1, 0, 0)}
+        for a in range(1, K_PASSES):
+            table[a] = load_table(streamed([P, T], U16), a)
+            w1_raw[a, 0] = load_weight(streamed([P, PACK, GROUP], F32), w1, a, 0)
+        load_scale_rows(w4_sc_raw, w4_scales)
 
         gs_wide = []
-        for b, width in enumerate((PAIRS, max(CHUNKS))):
-            gs_wide.append(keep.tile([P, PA1, width], F32, name="gs_wide%d" % b))
-            nc.scalar.copy(gs_wide[b][:], gs_sb[:, b, :].unsqueeze(2).to_broadcast([P, PA1, width]))
-        v_words = [keep.tile([P, S], U16, name="v_words%d" % a, align_bytes=64) for a in range(3)]
-        v_scales = [keep.tile([P, S], U8, name="v_scales%d" % a, align_bytes=64) for a in range(3)]
-        w1q = {}
+        for g, width in enumerate((PAIRS, HALF)):
+            gs_wide.append(keep.tile([P, PACK, width], F32, name="gs_wide%d" % g))
+            nc.scalar.copy(gs_wide[g][:], gs_sb[:, g, :].unsqueeze(2).to_broadcast([P, PACK, width]))
 
-        nc.vector.tensor_copy(v_words[0][:], tab0[:].indirect(offs_sb[:]))
-        nc.vector.tensor_copy(v_scales[0][:], tab_sc[:].indirect(offs_sb[:]))
-        d00 = round_weight(raw00, 0)
-        for a in (1, 2):
-            nc.scalar.dma_start(v_scales[a][0:100, :].bitcast(I32), v_scales[0][4 * a : 4 * a + 100, :].bitcast(I32))
-        nc.vector.tensor_copy(v_words[1][:], tab1[:].indirect(offs_sb[:]))
-        d10 = round_weight(raw10, 0)
-        w1q[0, 0] = quantize(d00, "w1q00")
-        w1q[1, 0] = quantize(d10, "w1q10")
-        nc.vector.tensor_copy(v_words[2][:], tab2[:].indirect(offs_sb[:]))
-        d20 = round_weight(raw20, 80)
-        w1q[2, 0] = quantize(d20, "w1q20")
+        v_words = [keep.tile([P, S], U16, name="v_words%d" % a, align_bytes=64) for a in range(K_PASSES)]
+        v_scales = [keep.tile([P, S], U8, name="v_scales%d" % a, align_bytes=64) for a in range(K_PASSES)]
+        w4_dealt = keep.tile([P, H_GROUPS, H], U16, name="w4_dealt", align_bytes=64)
+        w4_sc = [keep.tile([P, H], U8, name="w4_sc%d" % a, align_bytes=64) for a in range(H_GROUPS)]
 
-        w4_raw = big([P, 2, H], U16)
-        nc.sync.dma_start(w4_raw[:].bitcast(I32), w4_words.rearrange("a p c -> p a c").bitcast(I32))
-        pos1_sb = load_list(pos1, "pos1_sb")
-        pos2_sb = load_list(pos2, "pos2_sb")
-        raw1 = [load_rows(w1, a, 1) for a in range(3)]
-        for q in range(4):
-            nc.sync.dma_start(
-                w4_sc_raw[32 * q : 32 * q + 8, :].bitcast(I32), w4_scales[:, 4 * q : 4 * q + 4, :].bitcast(I32)
+        def deal_columns(dst, src):
+            nc.vector.tensor_copy(
+                dst.rearrange("p (g t q) -> p g t q", t=PACK, q=P), src.rearrange("p (g q t) -> p g t q", t=PACK, q=P)
             )
-        ge_sb = keep.tile([P, 2, PA1], F32, name="ge_sb")
-        nc.sync.dma_start(ge_sb[:], ge.rearrange("(b p t) -> p b t", p=P, t=PA1))
-        raw3 = [load_rows(w3, a, 0) for a in range(2)]
 
-        def first_pass(acc, a, b, t, s):
-            codes, scales = w1q[a, b]
+        def pick_words(a):
+            nc.vector.tensor_copy(v_words[a][:], table[a][:].indirect(offs_sb[:]))
+
+        for a in range(H_GROUPS):
+            deal_columns(w4_dealt[:, a, :], w4_raw[:, a, :])
+        pick_words(0)
+        nc.vector.tensor_copy(v_scales[0][:], tab_sc[:].indirect(offs_sb[:]))
+        for a in range(1, K_PASSES):
+            lift_scale_rows(v_scales[a], v_scales[0], a)
+        w1_dealt = {(0, 0): round_weight(w1_raw[0, 0])}
+        pick_words(1)
+        w1_dealt[1, 0] = round_weight(w1_raw[1, 0])
+        w1q = {(a, 0): quantize(w1_dealt[a, 0], "w1q%d0" % a) for a in range(2)}
+        pick_words(2)
+        w1_dealt[2, 0] = round_weight(w1_raw[2, 0], VECTOR_SHARE)
+        w1q[2, 0] = quantize(w1_dealt[2, 0], "w1q20")
+
+        for a in range(K_PASSES):
+            w1_raw[a, 1] = load_weight(streamed([P, PACK, GROUP], F32), w1, a, 1)
+        w3_raw = [load_weight(streamed([P, PACK, GROUP], F32), w3, a, 0) for a in range(H_GROUPS)]
+
+        sums = {}
+
+        def first_pass(a, g, t, s):
+            codes, scales = w1q[a, g]
             rows = slice(t * P, (t + 1) * P)
             cols = slice(s * BANK, (s + 1) * BANK)
             nc.tensor.matmul_mx(
-                out=acc[:],
+                out=sums[g, t, s][:],
                 lhsT=codes[:, rows].bitcast(FP8X4),
                 lhsT_scale=scales[:, rows],
                 rhs=v_words[a][:, cols].bitcast(FP4X4),
                 rhs_scale=v_scales[a][:, cols],
                 start=(a == 0),
-                stop=(a == 2),
+                stop=(a == K_PASSES - 1),
             )
 
-        acc1 = {}
-        for t in range(PA1):
+        for t in range(PACK):
             for s in range(2):
-                acc1[0, t, s] = bank()
-        for t in range(PA1):
-            for s in range(2):
-                first_pass(acc1[0, t, s], 0, 0, t, s)
-        for t in range(PA1):
-            for a in (1, 2):
+                sums[0, t, s] = bank()
+        for t in range(PACK):
+            for a in range(K_PASSES):
                 for s in range(2):
-                    first_pass(acc1[0, t, s], a, 0, t, s)
+                    first_pass(a, 0, t, s)
 
-        w3_dealt = keep.tile([P, 2 * PA1 * GROUP], BF16, name="w3_dealt", align_bytes=64)
+        def later_product(g, t):
+            for s in range(2):
+                sums[g, t, s] = bank()
+                for a in range(K_PASSES):
+                    first_pass(a, g, t, s)
 
-        def whole_tile(b, t):
-            if (b, t) == (1, 3):
+        slices = [(g, t) for g in range(H_GROUPS) for t in range(PACK)]
+        vector_only = slices[:VECTOR_ONLY_SLICES]
+        sines = {}
+        whole = {}
+        w3_dealt = keep.tile([P, H_GROUPS * PACK * GROUP], BF16, name="w3_dealt", align_bytes=64)
+
+        def whole_tile(g, t):
+            if (g, t) == slices[-1]:
                 return w3_dealt[:, S : 3 * S].bitcast(I32)
             return ring.tile([P, S], I32, name="whole", bufs=3, align_bytes=64)
 
-        h = {}
-        turns_int = {}
-
-        def product(b, t):
-            for s in range(2):
-                acc1[b, t, s] = bank()
-                for a in range(3):
-                    first_pass(acc1[b, t, s], a, b, t, s)
-
-        def turns(b, t):
-            h[b, t] = keep.tile([P, S], F32, name="h%d%d" % (b, t))
-            kind = RR[4 * b + t]
-            if kind == "A":
-                return
-            if kind == "C":
-                turns_int[b, t] = whole_tile(b, t)
+        def turns_on_scalar(g, t):
+            whole[g, t] = whole_tile(g, t)
             for s in range(2):
                 cols = slice(s * BANK, (s + 1) * BANK)
-                nc.scalar.activation(h[b, t][:, cols], acc1[b, t, s][:], ACT.Copy, scale=1.0 / TWO_PI)
-                if kind == "C":
-                    nc.scalar.activation(
-                        turns_int[b, t][:, cols].bitcast(U32), acc1[b, t, s][:], ACT.Copy, scale=1.0 / TWO_PI, bias=ROUNDER
-                    )
-
-        def whole_turns(b, t):
-            kind = RR[4 * b + t]
-            if kind == "C":
-                return
-            turns_int[b, t] = whole_tile(b, t)
-            if kind == "B":
-                nc.vector.tensor_copy(turns_int[b, t][:], h[b, t][:])
-            else:
-                for s in range(2):
-                    cols = slice(s * BANK, (s + 1) * BANK)
-                    nc.vector.tensor_scalar(turns_int[b, t][:, cols], acc1[b, t, s][:], 1.0 / TWO_PI, None, ALU.mult)
-
-        def fraction(b, t):
-            kind = RR[4 * b + t]
-            if kind == "B":
-                nc.vector.tensor_tensor(h[b, t][:], h[b, t][:], turns_int[b, t][:], ALU.subtract)
-            elif kind == "C":
-                nc.vector.scalar_tensor_tensor(
-                    h[b, t][:], turns_int[b, t][:], ROUNDER, h[b, t][:], ALU.subtract, ALU.subtract
+                nc.scalar.activation(sines[g, t][:, cols], sums[g, t, s][:], ACT.Copy, scale=1.0 / TWO_PI)
+                nc.scalar.activation(
+                    whole[g, t][:, cols].bitcast(U32), sums[g, t, s][:], ACT.Copy, scale=1.0 / TWO_PI, bias=ROUNDER
                 )
-            else:
-                for s in range(2):
-                    cols = slice(s * BANK, (s + 1) * BANK)
-                    nc.vector.scalar_tensor_tensor(
-                        h[b, t][:, cols], acc1[b, t, s][:], 1.0 / TWO_PI, turns_int[b, t][:, cols], ALU.mult, ALU.subtract
-                    )
 
-        def sine(b, t):
-            sign = -1.0 if RR[4 * b + t] == "C" else 1.0
-            nc.scalar.activation(h[b, t][:], h[b, t][:], ACT.Sin, scale=sign * TWO_PI)
+        def reduce_turns(g, t):
+            if (g, t) not in vector_only:
+                nc.vector.scalar_tensor_tensor(
+                    sines[g, t][:], whole[g, t][:], ROUNDER, sines[g, t][:], ALU.subtract, ALU.subtract
+                )
+                return
+            whole[g, t] = whole_tile(g, t)
+            halves = [(s, slice(s * BANK, (s + 1) * BANK)) for s in range(2)]
+            for s, cols in halves:
+                nc.vector.tensor_scalar(whole[g, t][:, cols], sums[g, t, s][:], 1.0 / TWO_PI, None, ALU.mult)
+            for s, cols in halves:
+                nc.vector.scalar_tensor_tensor(
+                    sines[g, t][:, cols], sums[g, t, s][:], 1.0 / TWO_PI, whole[g, t][:, cols], ALU.mult, ALU.subtract
+                )
 
-        last = len(CHUNKS) - 1
-        cur = {}
-        arc = {}
-        top = {}
-        cur[0, 0] = keep.tile([P, PA1, PAIRS], F32, name="cur0")[:]
-        arc[0, 0] = keep.tile([P, PA1, PAIRS], F32, name="arc0")[:]
-        cur1 = keep.tile([P, PA1 * max(CHUNKS)], F32, name="cur1")
-        arc1 = keep.tile([P, PA1 * max(CHUNKS)], F32, name="arc1")
-        for u, width in enumerate(CHUNKS):
-            cur[1, u] = cur1[:, : PA1 * width].rearrange("p (t j) -> p t j", t=PA1)
-            arc[1, u] = arc1[:, : PA1 * width].rearrange("p (t j) -> p t j", t=PA1)
-            top[1, u] = cur[1, u] if u == last else keep.tile([P, PA1, width], F32, name="top%d" % u)[:]
+        def sine(g, t):
+            scale = TWO_PI if (g, t) in vector_only else -TWO_PI
+            nc.scalar.activation(sines[g, t][:], sines[g, t][:], ACT.Sin, scale=scale)
 
-        def pick(b, t, u):
-            first = STARTS[u] // 16
-            part = slice(first, first + cur[b, u].shape[2] // 16)
-            gains = gs_wide[b][:, t, : cur[b, u].shape[2]]
-            nc.vector.tensor_tensor(cur[b, u][:, t, :], h[b, t][:].indirect(pos1_sb[:, part]), gains, ALU.mult)
-            nc.vector.tensor_tensor(arc[b, u][:, t, :], h[b, t][:].indirect(pos2_sb[:, part]), gains, ALU.mult)
+        cur_first = keep.tile([P, PACK, PAIRS], F32, name="cur_first", align_bytes=64)
+        arc_first = keep.tile([P, PACK, PAIRS], F32, name="arc_first", align_bytes=64)
+        cur_second = keep.tile([P, PACK, HALF], F32, name="cur_second")
+        arc_second = keep.tile([P, PACK, HALF], F32, name="arc_second")
+        cur = [cur_first, cur_second]
+        arc = [arc_first, arc_second]
+        top_second = keep.tile([P, PACK, HALF], F32, name="w4_raw", align_bytes=64)
+        shared = keep.tile([P, PACK * HALF], F32, name="tab_sc", align_bytes=64)
+        top = {
+            (0, 0): cur_first[:, :, :HALF],
+            (0, 1): shared[:].rearrange("p (t j) -> p t j", t=PACK),
+            (1, 0): top_second[:],
+            (1, 1): cur_second[:],
+        }
 
-        d3 = {}
-        dl = {}
-        dlq = {}
+        def pick(g, t, u):
+            width = cur[g].shape[2]
+            part = slice(u * width // 16, (u + 1) * width // 16)
+            for picked, offsets in ((cur[g], pos1_sb), (arc[g], pos2_sb)):
+                nc.vector.tensor_tensor(
+                    picked[:, t, :], sines[g, t][:].indirect(offsets[:, part]), gs_wide[g][:, t, :], ALU.mult
+                )
 
-        def difference(b, u):
-            width = cur[b, u].shape[2]
-            dl[b, u] = ring.tile([P, PA1 * width], BF16, name="dl", align_bytes=64)
-            nc.vector.tensor_tensor(woven(dl[b, u][:], RUN), planar(cur[b, u], RUN), planar(arc[b, u], RUN), ALU.subtract)
+        def difference(g, dl=None):
+            if dl is None:
+                dl = ring.tile([P, PACK * cur[g].shape[2]], BF16, name="dl", align_bytes=64)
+            nc.vector.tensor_tensor(woven(dl[:], 2), planar(cur[g][:], 2), planar(arc[g][:], 2), ALU.subtract)
+            return dl
 
-        def larger(b, u):
-            nc.vector.tensor_tensor(top[b, u], cur[b, u], arc[b, u], ALU.max)
+        def larger(g, u):
+            cols = slice(u * HALF, (u + 1) * HALF) if g == 0 else slice(0, HALF)
+            nc.vector.tensor_tensor(top[g, u], cur[g][:, :, cols], arc[g][:, :, cols], ALU.max)
 
-        def larger_first(u):
-            cols = slice(STARTS[u], STARTS[u] + CHUNKS[u])
-            nc.vector.tensor_tensor(top[0, u], cur[0, 0][:, :, cols], arc[0, 0][:, :, cols], ALU.max)
-
-        w4_dealt = keep.tile([P, 2, H], U16, name="w4_dealt", align_bytes=64)
-        w4_sc = [keep.tile([P, H], U8, name="w4_sc%d" % a, align_bytes=64) for a in range(2)]
-
-        def deal_w4_words(a):
-            nc.vector.tensor_copy(
-                w4_dealt[:, a, :].rearrange("p (b t q) -> p b t q", t=PA1, q=P),
-                w4_raw[:, a, :].rearrange("p (b q t) -> p b t q", t=PA1, q=P),
-            )
-
-        def deal_w4_scales():
-            nc.vector.tensor_copy(
-                w4_sc[0][:].rearrange("p (b t q) -> p b t q", t=PA1, q=P),
-                w4_sc_raw[:].rearrange("p (b q t) -> p b t q", t=PA1, q=P),
-            )
-            nc.scalar.dma_start(w4_sc[1][0:100, :].bitcast(I32), w4_sc[0][4:104, :].bitcast(I32))
-
-        tiles = [(b, t) for b in range(2) for t in range(PA1)]
-        d1 = {}
-        for k in range(len(tiles) + 2):
-            if 1 <= k <= len(tiles):
-                sine(*tiles[k - 1])
-            if 1 + 1 <= k <= 1 + 3:
-                w1q[k - 1 - 1, 1] = quantize(d1[k - 1 - 1], "w1q%d1" % (k - 1 - 1))
-            if False and 1 <= k <= 1 + 2:
-                d1[k - 1] = round_weight(raw1[k - 1], 0)
-            if k < len(tiles):
-                if k >= PA1:
-                    product(*tiles[k])
-                turns(*tiles[k])
-            if not False and 1 <= k <= 1 + 2:
-                d1[k - 1] = round_weight(raw1[k - 1], 0)
-            if k < len(tiles):
-                whole_turns(*tiles[k])
-                fraction(*tiles[k])
+        for k in range(len(slices) + 2):
+            if 1 <= k <= K_PASSES:
+                w1q[k - 1, 1] = quantize(w1_dealt[k - 1, 1], "w1q%d1" % (k - 1))
+            if k < K_PASSES:
+                w1_dealt[k, 1] = round_weight(w1_raw[k, 1])
+            if k < len(slices):
+                g, t = slices[k]
+                if g > 0:
+                    later_product(g, t)
+                sines[g, t] = keep.tile([P, S], F32, name="sines%d%d" % (g, t))
+                if (g, t) not in vector_only:
+                    turns_on_scalar(g, t)
+            if 1 <= k <= len(slices):
+                sine(*slices[k - 1])
+            if k < len(slices):
+                reduce_turns(*slices[k])
             if k >= 2:
-                pick(*tiles[k - 2], 0)
-            if k < 2:
-                deal_w4_words(k)
-            if k == 2:
-                deal_w4_scales()
-            if k == 5:
-                difference(0, 0)
-            if k == 6:
-                dlq[0, 0] = quantize(dl[0, 0], "dlq00")
+                pick(*slices[k - 2], 0)
+            if k == 0:
+                deal_columns(w4_sc[0][:], w4_sc_raw[:])
+                lift_scale_rows(w4_sc[1], w4_sc[0], 1)
+            if k == PACK + 1:
+                dl_first = difference(0)
+            if k == PACK + 2:
+                dlq_first = quantize(dl_first, "dlq_first")
 
-        for a in range(2):
-            d3[a] = round_weight(raw3[a], 0, w3_dealt[:, a * PA1 * GROUP : (a + 1) * PA1 * GROUP])
+        w3_parts = [w3_dealt[:, a * PACK * GROUP : (a + 1) * PACK * GROUP] for a in range(H_GROUPS)]
+        for a in range(H_GROUPS):
+            round_weight(w3_raw[a], dealt=w3_parts[a])
 
-        e = {}
+        gained = {}
 
-        def second_stage(u):
-            width = CHUNKS[u]
-            share = BANK // width
-            for b in range(2):
-                e[b, u] = ring.tile([P, PA1, width], F32, name="e", bufs=4)
-                for t0 in range(0, PA1, share):
+        def second_stage(u, dlq_second):
+            for g in range(H_GROUPS):
+                gained[g, u] = ring.tile([P, PACK, HALF], F32, name="gained", bufs=3)
+                for t0 in range(0, PACK, 2):
                     acc = bank()
-                    for i in range(share):
-                        t = t0 + i
-                        rows = slice((b * PA1 + t) * P, (b * PA1 + t + 1) * P)
-                        for q in range(0, width, P):
-                            for a in range(2):
-                                codes, scales = dlq[0, 0] if a == 0 else dlq[1, u]
-                                first = q + (STARTS[u] if a == 0 else 0)
-                                cols = slice(first, first + P)
+                    for i in range(2):
+                        rows = slice((g * PACK + t0 + i) * P, (g * PACK + t0 + i + 1) * P)
+                        for c in range(0, HALF, P):
+                            for a, (codes, scales), first in ((0, dlq_first, u * HALF + c), (1, dlq_second, c)):
                                 nc.tensor.matmul_mx(
-                                    out=acc[:, i * width + q : i * width + q + P],
+                                    out=acc[:, i * HALF + c : i * HALF + c + P],
                                     lhsT=w4_dealt[:, a, rows].bitcast(FP4X4),
                                     lhsT_scale=w4_sc[a][:, rows],
-                                    rhs=codes[:, cols].bitcast(FP8X4),
-                                    rhs_scale=scales[:, cols],
+                                    rhs=codes[:, first : first + P].bitcast(FP8X4),
+                                    rhs_scale=scales[:, first : first + P],
                                     start=(a == 0),
                                     stop=(a == 1),
                                 )
                     nc.scalar.activation(
-                        e[b, u][:, t0 : t0 + share, :].rearrange("p t j -> p (t j)"), acc[:], ACT.Tanh
+                        gained[g, u][:, t0 : t0 + 2, :].rearrange("p t j -> p (t j)"), acc[:], ACT.Tanh
                     )
-                    if u not in GEV:
-                        for t in range(t0, t0 + share):
-                            nc.scalar.activation(
-                                e[b, u][:, t, :], e[b, u][:, t, :], ACT.Copy, scale=ge_sb[:, b, t : t + 1]
-                            )
-
-        z = {}
-        zq = {}
-
-        def blend(b, u):
-            width = CHUNKS[u]
-            z[b, u] = ring.tile([P, PA1 * width], BF16, name="z", bufs=3, align_bytes=64)
-            best = top[b, u]
-            if u in GEV:
-                gains = ge_sb[:, b, :].unsqueeze(2).to_broadcast([P, PA1, width])
-                nc.vector.tensor_tensor(e[b, u][:], e[b, u][:], gains, ALU.mult)
-            nc.vector.tensor_tensor(woven(z[b, u][:], RUN), planar(e[b, u][:], RUN), planar(best, RUN), ALU.add)
+                    for t in (t0, t0 + 1):
+                        nc.scalar.activation(
+                            gained[g, u][:, t, :], gained[g, u][:, t, :], ACT.Copy, scale=ge_sb[:, g, t : t + 1]
+                        )
 
         y_codes = keep.tile([P, PAIRS], U32, name="y_codes", align_bytes=64)
         y_scales = keep.tile([P, PAIRS], U8, name="y_scales", align_bytes=64)
         y = {}
-        y16 = {}
         w3q = {}
 
-        def third_stage(u):
-            width = CHUNKS[u]
-            share = BANK // width
-            y[u] = ring.tile([P, PA1, width], F32, name="y")
-            for t0 in range(0, PA1, share):
-                acc = bank()
-                for i in range(share):
-                    rows = slice((t0 + i) * P, (t0 + i + 1) * P)
-                    for a in range(2):
-                        nc.tensor.matmul_mx(
-                            out=acc[:, i * width : (i + 1) * width],
-                            lhsT=w3q[a][0][:, rows].bitcast(FP8X4),
-                            lhsT_scale=w3q[a][1][:, rows],
-                            rhs=zq[a, u][0][:].bitcast(FP8X4),
-                            rhs_scale=zq[a, u][1][:],
-                            start=(a == 0),
-                            stop=(a == 1),
-                        )
-                nc.scalar.copy(y[u][:, t0 : t0 + share, :].rearrange("p t j -> p (t j)"), acc[:])
-            nc.sync.dma_start(out_0.rearrange("(p t) j -> p t j", t=PA1)[:, :, STARTS[u] : STARTS[u] + width], y[u][:])
+        def blend(g, u, c, width):
+            z = ring.tile([P, PACK * width], BF16, name="z", bufs=3, align_bytes=64)
+            cols = slice(c, c + width)
+            nc.vector.tensor_tensor(
+                woven(z[:], 2), planar(gained[g, u][:, :, cols], 2), planar(top[g, u][:, :, cols], 2), ALU.add
+            )
+            return z
 
-        def round_result(u):
-            y16[u] = ring.tile([P, PA1 * CHUNKS[u]], BF16, name="y16", align_bytes=64)
-            if u in Y16S:
-                nc.scalar.copy(woven(y16[u][:], 4), planar(y[u][:], 4))
-            else:
-                nc.vector.tensor_copy(woven(y16[u][:], 4), planar(y[u][:], 4))
+        def third_stage(u):
+            for c, width in PIECES[u]:
+                z = [blend(g, u, c, width) for g in range(H_GROUPS)]
+                zq = [quantize(z[g], "zq%d%d%d" % (g, u, c)) for g in range(H_GROUPS)]
+                per_bank = BANK // width
+                y[u, c] = ring.tile([P, PACK, width], F32, name="y", bufs=3)
+                for t0 in range(0, PACK, per_bank):
+                    acc = bank()
+                    for i in range(per_bank):
+                        rows = slice((t0 + i) * P, (t0 + i + 1) * P)
+                        for a in range(H_GROUPS):
+                            nc.tensor.matmul_mx(
+                                out=acc[:, i * width : (i + 1) * width],
+                                lhsT=w3q[a][0][:, rows].bitcast(FP8X4),
+                                lhsT_scale=w3q[a][1][:, rows],
+                                rhs=zq[a][0][:].bitcast(FP8X4),
+                                rhs_scale=zq[a][1][:],
+                                start=(a == 0),
+                                stop=(a == H_GROUPS - 1),
+                            )
+                    nc.scalar.copy(y[u, c][:, t0 : t0 + per_bank, :].rearrange("p t j -> p (t j)"), acc[:])
+                first = u * HALF + c
+                nc.sync.dma_start(
+                    out_0.rearrange("(p t) j -> p t j", t=PACK)[:, :, first : first + width], y[u, c][:]
+                )
 
         def planes(u):
-            cols = slice(STARTS[u], STARTS[u] + CHUNKS[u])
-            nc.vector.quantize_mx(out=y_codes[:, cols].bitcast(FP8X4), scales=y_scales[:, cols], in_=y16[u][:])
-            nc.sync.dma_start(
-                out_1[0].rearrange("p m t -> p (m t)").bitcast(I32)[:, cols], y_codes[:, cols].bitcast(I32)
-            )
+            for c, width in PIECES[u]:
+                y16 = ring.tile([P, PACK * width], BF16, name="y16", align_bytes=64)
+                if u * HALF + c + width == PAIRS:
+                    nc.vector.tensor_copy(woven(y16[:], 4), planar(y[u, c][:], 4))
+                else:
+                    nc.scalar.copy(woven(y16[:], 4), planar(y[u, c][:], 4))
+                cols = slice(u * HALF + c, u * HALF + c + width)
+                nc.vector.quantize_mx(out=y_codes[:, cols].bitcast(FP8X4), scales=y_scales[:, cols], in_=y16[:])
+                nc.sync.dma_start(
+                    out_1[0].rearrange("p m t -> p (m t)").bitcast(I32)[:, cols], y_codes[:, cols].bitcast(I32)
+                )
 
-        for u in range(last + 3):
-            if 1 <= u <= last:
-                for t in range(PA1):
-                    pick(1, t, u)
-            if u <= last:
-                difference(1, u)
-                if u < last:
-                    larger(1, u)
-                if u == 1:
-                    w3q[0] = quantize(d3[0], "w3q0")
-                dlq[1, u] = quantize(dl[1, u], "dlq1%d" % u)
-                second_stage(u)
-                top[0, u] = cur[0, 0][:, :, STARTS[u] : STARTS[u] + CHUNKS[u]]
-                larger_first(u)
-                if u == 1:
-                    w3q[1] = quantize(d3[1], "w3q1")
-                if u == last:
-                    larger(1, u)
-            if 1 <= u <= last + 1:
-                blend(0, u - 1)
-                blend(1, u - 1)
-                zq[0, u - 1] = quantize(z[0, u - 1], "zq0%d" % u)
-                zq[1, u - 1] = quantize(z[1, u - 1], "zq1%d" % u)
-                third_stage(u - 1)
-            if u >= 2:
-                round_result(u - 2)
-                planes(u - 2)
-        for q in range(4):
+        dl_half = difference(1)
+        larger(1, 0)
+        second_stage(0, quantize(dl_half, "dlq_half0"))
+        larger(0, 0)
+
+        for t in range(PACK):
+            pick(1, t, 1)
+        dl_half = difference(1, shared[:].bitcast(BF16)[:, : PACK * HALF])
+        w3q[0] = quantize(w3_parts[0], "w3q0")
+        second_stage(1, quantize(dl_half, "dlq_half1"))
+        larger(0, 1)
+        w3q[1] = quantize(w3_parts[1], "w3q1")
+        larger(1, 1)
+
+        third_stage(0)
+        third_stage(1)
+        planes(0)
+        planes(1)
+        for q in range(QUADRANTS):
             queue = nc.sync if q % 2 == 0 else nc.scalar
             queue.dma_start(out_2[0, 4 * q : 4 * q + 4, :].bitcast(I32), y_scales[32 * q : 32 * q + 4, :].bitcast(I32))

import math
from contextlib import ExitStack

import concourse.mybir as mybir

K, T, S, PAIRS, H, N = 1536, 4096, 1024, 512, 1024, 512
FLOPS = 2 * (K * H * S + H * H * PAIRS + H * N * PAIRS)

F32 = mybir.dt.float32
BF16 = mybir.dt.bfloat16
I32 = mybir.dt.int32
U32 = mybir.dt.uint32
U16 = mybir.dt.uint16
U8 = mybir.dt.uint8
FP8X4 = mybir.dt.float8_e4m3fn_x4
FP4X4 = mybir.dt.float4_e2m1fn_x4
ACT = mybir.ActivationFunctionType
ALU = mybir.AluOpType

P = 128
PACK = 4
GROUP = P * PACK
BANK = 512
HALF = PAIRS // 2
K_PASSES = K // GROUP
H_GROUPS = H // GROUP
QUADRANTS = 4
SCALE_SPAN = 100
TWO_PI = 2.0 * math.pi
ROUNDER = 1.5 * 2.0**23

VECTOR_ONLY_SLICES = 2
VECTOR_SHARE = 80
PIECES = {0: [(0, HALF)], 1: [(0, P), (P, P)]}


def tile_list_tile_lot_joining_kernel(
    tc, tab_words, tab_scales, offs, pos1, pos2, w1, gs, w4_words, w4_scales, ge, w3, out_0, out_1, out_2
):
    nc = tc.nc
    with ExitStack() as ctx:
        keep = ctx.enter_context(tc.tile_pool(name="keep", bufs=1))
        ring = ctx.enter_context(tc.tile_pool(name="ring", bufs=2))
        psum = ctx.enter_context(tc.psum_pool(name="psum", bufs=8))

        def bank():
            return psum.tile([P, BANK], F32, name="bank")

        def streamed(shape, dtype):
            return ring.tile(shape, dtype, name="streamed", bufs=4, align_bytes=64)

        def load_list(src, name):
            offsets = keep.tile([P, src.shape[1]], U16, name=name)
            nc.sync.dma_start(offsets[:], src)
            return offsets

        def load_gain(src, name):
            gain = keep.tile([P, H_GROUPS, PACK], F32, name=name)
            nc.sync.dma_start(gain[:], src.rearrange("(g p t) -> p g t", p=P, t=PACK))
            return gain

        def load_weight(raw, w, a, g):
            block = w[a * GROUP : (a + 1) * GROUP, g * GROUP : (g + 1) * GROUP]
            nc.sync.dma_start(raw[:], block.rearrange("(p j) c -> p j c", j=PACK))
            return raw

        def load_table(words, a):
            nc.sync.dma_start(words[:].bitcast(I32), tab_words[a].bitcast(I32))
            return words

        def load_scale_rows(rows, src):
            live = 4 * src.shape[0]
            for q in range(QUADRANTS):
                nc.sync.dma_start(rows[32 * q : 32 * q + live, :].bitcast(I32), src[:, 4 * q : 4 * q + 4, :].bitcast(I32))

        def lift_scale_rows(dst, packed, a):
            nc.sync.dma_start(dst[0:SCALE_SPAN, :].bitcast(I32), packed[4 * a : 4 * a + SCALE_SPAN, :].bitcast(I32))

        def round_weight(raw, vector_share=0, dealt=None):
            if dealt is None:
                dealt = ring.tile([P, PACK * GROUP], BF16, name="dealt", bufs=3, align_bytes=64)
            dst = dealt[:].rearrange("p (t m j) -> p m t j", t=PACK, j=PACK)
            src = raw[:].rearrange("p j (m t) -> p m t j", t=PACK)
            nc.scalar.copy(dst[:, vector_share:], src[:, vector_share:])
            if vector_share:
                nc.vector.tensor_copy(dst[:, :vector_share], src[:, :vector_share])
            return dealt

        def quantize(values, name):
            width = values.shape[1] // PACK
            codes = keep.tile([P, width], U32, name=name + "_codes", align_bytes=64)
            scales = keep.tile([P, width], U8, name=name + "_scales", align_bytes=64)
            nc.vector.quantize_mx(out=codes[:].bitcast(FP8X4), scales=scales[:], in_=values[:])
            return codes, scales

        def woven(flat, run):
            return flat.rearrange("p (c i t) -> p c t i", i=run, t=PACK)

        def planar(rows, run):
            return rows.rearrange("p t (c i) -> p c t i", i=run)

        offs_sb = load_list(offs, "offs_sb")
        gs_sb = load_gain(gs, "gs_sb")
        pos1_sb = load_list(pos1, "pos1_sb")
        pos2_sb = load_list(pos2, "pos2_sb")
        ge_sb = load_gain(ge, "ge_sb")
        tab_sc = keep.tile([P, T], U8, name="tab_sc", align_bytes=64)
        nc.vector.memset(tab_sc[:].bitcast(I32), 0)
        w4_sc_raw = keep.tile([P, H], U8, name="w4_sc_raw", align_bytes=64)
        nc.vector.memset(w4_sc_raw[:].bitcast(I32), 0)
        warm = keep.tile([P, 8], F32, name="warm")
        nc.vector.memset(warm[:], 0.0)
        nc.scalar.activation(warm[:], warm[:], ACT.Silu)
        w4_raw = keep.tile([P, H_GROUPS, H], U16, name="w4_raw", align_bytes=64)
        nc.sync.dma_start(w4_raw[:].bitcast(I32), w4_words.rearrange("a p c -> p a c").bitcast(I32))
        table = {0: load_table(keep.tile([P, T], U16, name="cur_first", align_bytes=64), 0)}
        load_scale_rows(tab_sc, tab_scales)
        w1_raw = {(0, 0): load_weight(keep.tile([P, PACK, GROUP], F32, name="arc_first", align_bytes=64), w1, 0, 0)}
        for a in range(1, K_PASSES):
            table[a] = load_table(streamed([P, T], U16), a)
            w1_raw[a, 0] = load_weight(streamed([P, PACK, GROUP], F32), w1, a, 0)
        load_scale_rows(w4_sc_raw, w4_scales)

        gs_wide = []
        for g, width in enumerate((PAIRS, HALF)):
            gs_wide.append(keep.tile([P, PACK, width], F32, name="gs_wide%d" % g))
            nc.scalar.copy(gs_wide[g][:], gs_sb[:, g, :].unsqueeze(2).to_broadcast([P, PACK, width]))

        v_words = [keep.tile([P, S], U16, name="v_words%d" % a, align_bytes=64) for a in range(K_PASSES)]
        v_scales = [keep.tile([P, S], U8, name="v_scales%d" % a, align_bytes=64) for a in range(K_PASSES)]
        w4_dealt = keep.tile([P, H_GROUPS, H], U16, name="w4_dealt", align_bytes=64)
        w4_sc = [keep.tile([P, H], U8, name="w4_sc%d" % a, align_bytes=64) for a in range(H_GROUPS)]

        def deal_columns(dst, src):
            nc.vector.tensor_copy(
                dst.rearrange("p (g t q) -> p g t q", t=PACK, q=P), src.rearrange("p (g q t) -> p g t q", t=PACK, q=P)
            )

        def pick_words(a):
            nc.vector.tensor_copy(v_words[a][:], table[a][:].indirect(offs_sb[:]))

        for a in range(H_GROUPS):
            deal_columns(w4_dealt[:, a, :], w4_raw[:, a, :])
        pick_words(0)
        nc.vector.tensor_copy(v_scales[0][:], tab_sc[:].indirect(offs_sb[:]))
        for a in range(1, K_PASSES):
            lift_scale_rows(v_scales[a], v_scales[0], a)
        w1_dealt = {(0, 0): round_weight(w1_raw[0, 0])}
        pick_words(1)
        w1_dealt[1, 0] = round_weight(w1_raw[1, 0])
        w1q = {(a, 0): quantize(w1_dealt[a, 0], "w1q%d0" % a) for a in range(2)}
        pick_words(2)
        w1_dealt[2, 0] = round_weight(w1_raw[2, 0], VECTOR_SHARE)
        w1q[2, 0] = quantize(w1_dealt[2, 0], "w1q20")

        for a in range(K_PASSES):
            w1_raw[a, 1] = load_weight(streamed([P, PACK, GROUP], F32), w1, a, 1)
        w3_raw = [load_weight(streamed([P, PACK, GROUP], F32), w3, a, 0) for a in range(H_GROUPS)]

        sums = {}

        def first_pass(a, g, t, s):
            codes, scales = w1q[a, g]
            rows = slice(t * P, (t + 1) * P)
            cols = slice(s * BANK, (s + 1) * BANK)
            nc.tensor.matmul_mx(
                out=sums[g, t, s][:],
                lhsT=codes[:, rows].bitcast(FP8X4),
                lhsT_scale=scales[:, rows],
                rhs=v_words[a][:, cols].bitcast(FP4X4),
                rhs_scale=v_scales[a][:, cols],
                start=(a == 0),
                stop=(a == K_PASSES - 1),
            )

        for t in range(PACK):
            for s in range(2):
                sums[0, t, s] = bank()
        for t in range(PACK):
            for a in range(K_PASSES):
                for s in range(2):
                    first_pass(a, 0, t, s)

        def later_product(g, t):
            for s in range(2):
                sums[g, t, s] = bank()
                for a in range(K_PASSES):
                    first_pass(a, g, t, s)

        slices = [(g, t) for g in range(H_GROUPS) for t in range(PACK)]
        vector_only = slices[:VECTOR_ONLY_SLICES]
        sines = {}
        whole = {}
        w3_dealt = keep.tile([P, H_GROUPS * PACK * GROUP], BF16, name="w3_dealt", align_bytes=64)

        def whole_tile(g, t):
            if (g, t) == slices[-1]:
                return w3_dealt[:, S : 3 * S].bitcast(I32)
            return ring.tile([P, S], I32, name="whole", bufs=3, align_bytes=64)

        def turns_on_scalar(g, t):
            whole[g, t] = whole_tile(g, t)
            for s in range(2):
                cols = slice(s * BANK, (s + 1) * BANK)
                nc.scalar.activation(sines[g, t][:, cols], sums[g, t, s][:], ACT.Copy, scale=1.0 / TWO_PI)
                nc.scalar.activation(
                    whole[g, t][:, cols].bitcast(U32), sums[g, t, s][:], ACT.Copy, scale=1.0 / TWO_PI, bias=ROUNDER
                )

        def reduce_turns(g, t):
            if (g, t) not in vector_only:
                nc.vector.scalar_tensor_tensor(
                    sines[g, t][:], whole[g, t][:], ROUNDER, sines[g, t][:], ALU.subtract, ALU.subtract
                )
                return
            whole[g, t] = whole_tile(g, t)
            halves = [(s, slice(s * BANK, (s + 1) * BANK)) for s in range(2)]
            for s, cols in halves:
                nc.vector.tensor_scalar(whole[g, t][:, cols], sums[g, t, s][:], 1.0 / TWO_PI, None, ALU.mult)
            for s, cols in halves:
                nc.vector.scalar_tensor_tensor(
                    sines[g, t][:, cols], sums[g, t, s][:], 1.0 / TWO_PI, whole[g, t][:, cols], ALU.mult, ALU.subtract
                )

        def sine(g, t):
            scale = TWO_PI if (g, t) in vector_only else -TWO_PI
            nc.scalar.activation(sines[g, t][:], sines[g, t][:], ACT.Sin, scale=scale)

        cur_first = keep.tile([P, PACK, PAIRS], F32, name="cur_first", align_bytes=64)
        arc_first = keep.tile([P, PACK, PAIRS], F32, name="arc_first", align_bytes=64)
        cur_second = keep.tile([P, PACK, HALF], F32, name="cur_second")
        arc_second = keep.tile([P, PACK, HALF], F32, name="arc_second")
        cur = [cur_first, cur_second]
        arc = [arc_first, arc_second]
        top_second = keep.tile([P, PACK, HALF], F32, name="w4_raw", align_bytes=64)
        shared = keep.tile([P, PACK * HALF], F32, name="tab_sc", align_bytes=64)
        top = {
            (0, 0): cur_first[:, :, :HALF],
            (0, 1): shared[:].rearrange("p (t j) -> p t j", t=PACK),
            (1, 0): top_second[:],
            (1, 1): cur_second[:],
        }

        def pick(g, t, u):
            width = cur[g].shape[2]
            part = slice(u * width // 16, (u + 1) * width // 16)
            for picked, offsets in ((cur[g], pos1_sb), (arc[g], pos2_sb)):
                nc.vector.tensor_tensor(
                    picked[:, t, :], sines[g, t][:].indirect(offsets[:, part]), gs_wide[g][:, t, :], ALU.mult
                )

        def difference(g, dl=None):
            if dl is None:
                dl = ring.tile([P, PACK * cur[g].shape[2]], BF16, name="dl", align_bytes=64)
            nc.vector.tensor_tensor(woven(dl[:], 2), planar(cur[g][:], 2), planar(arc[g][:], 2), ALU.subtract)
            return dl

        def larger(g, u):
            cols = slice(u * HALF, (u + 1) * HALF) if g == 0 else slice(0, HALF)
            nc.vector.tensor_tensor(top[g, u], cur[g][:, :, cols], arc[g][:, :, cols], ALU.max)

        for k in range(len(slices) + 2):
            if 1 <= k <= K_PASSES:
                w1q[k - 1, 1] = quantize(w1_dealt[k - 1, 1], "w1q%d1" % (k - 1))
            if k < K_PASSES:
                w1_dealt[k, 1] = round_weight(w1_raw[k, 1])
            if k < len(slices):
                g, t = slices[k]
                if g > 0:
                    later_product(g, t)
                sines[g, t] = keep.tile([P, S], F32, name="sines%d%d" % (g, t))
                if (g, t) not in vector_only:
                    turns_on_scalar(g, t)
            if 1 <= k <= len(slices):
                sine(*slices[k - 1])
            if k < len(slices):
                reduce_turns(*slices[k])
            if k >= 2:
                pick(*slices[k - 2], 0)
            if k == 0:
                deal_columns(w4_sc[0][:], w4_sc_raw[:])
                lift_scale_rows(w4_sc[1], w4_sc[0], 1)
            if k == PACK + 1:
                dl_first = difference(0)
            if k == PACK + 2:
                dlq_first = quantize(dl_first, "dlq_first")

        w3_parts = [w3_dealt[:, a * PACK * GROUP : (a + 1) * PACK * GROUP] for a in range(H_GROUPS)]
        for a in range(H_GROUPS):
            round_weight(w3_raw[a], dealt=w3_parts[a])

        gained = {}

        def second_stage(u, dlq_second):
            for g in range(H_GROUPS):
                gained[g, u] = ring.tile([P, PACK, HALF], F32, name="gained", bufs=3)
                for t0 in range(0, PACK, 2):
                    acc = bank()
                    for i in range(2):
                        rows = slice((g * PACK + t0 + i) * P, (g * PACK + t0 + i + 1) * P)
                        for c in range(0, HALF, P):
                            for a, (codes, scales), first in ((0, dlq_first, u * HALF + c), (1, dlq_second, c)):
                                nc.tensor.matmul_mx(
                                    out=acc[:, i * HALF + c : i * HALF + c + P],
                                    lhsT=w4_dealt[:, a, rows].bitcast(FP4X4),
                                    lhsT_scale=w4_sc[a][:, rows],
                                    rhs=codes[:, first : first + P].bitcast(FP8X4),
                                    rhs_scale=scales[:, first : first + P],
                                    start=(a == 0),
                                    stop=(a == 1),
                                )
                    nc.scalar.activation(
                        gained[g, u][:, t0 : t0 + 2, :].rearrange("p t j -> p (t j)"), acc[:], ACT.Tanh
                    )
                    for t in (t0, t0 + 1):
                        nc.scalar.activation(
                            gained[g, u][:, t, :], gained[g, u][:, t, :], ACT.Copy, scale=ge_sb[:, g, t : t + 1]
                        )

        y_codes = keep.tile([P, PAIRS], U32, name="y_codes", align_bytes=64)
        y_scales = keep.tile([P, PAIRS], U8, name="y_scales", align_bytes=64)
        y = {}
        w3q = {}

        def blend(g, u, c, width):
            z = ring.tile([P, PACK * width], BF16, name="z", bufs=3, align_bytes=64)
            cols = slice(c, c + width)
            nc.vector.tensor_tensor(
                woven(z[:], 2), planar(gained[g, u][:, :, cols], 2), planar(top[g, u][:, :, cols], 2), ALU.add
            )
            return z

        def third_stage(u):
            for c, width in PIECES[u]:
                z = [blend(g, u, c, width) for g in range(H_GROUPS)]
                zq = [quantize(z[g], "zq%d%d%d" % (g, u, c)) for g in range(H_GROUPS)]
                per_bank = BANK // width
                y[u, c] = ring.tile([P, PACK, width], F32, name="y", bufs=3)
                for t0 in range(0, PACK, per_bank):
                    acc = bank()
                    for i in range(per_bank):
                        rows = slice((t0 + i) * P, (t0 + i + 1) * P)
                        for a in range(H_GROUPS):
                            nc.tensor.matmul_mx(
                                out=acc[:, i * width : (i + 1) * width],
                                lhsT=w3q[a][0][:, rows].bitcast(FP8X4),
                                lhsT_scale=w3q[a][1][:, rows],
                                rhs=zq[a][0][:].bitcast(FP8X4),
                                rhs_scale=zq[a][1][:],
                                start=(a == 0),
                                stop=(a == H_GROUPS - 1),
                            )
                    nc.scalar.copy(y[u, c][:, t0 : t0 + per_bank, :].rearrange("p t j -> p (t j)"), acc[:])
                first = u * HALF + c
                nc.sync.dma_start(
                    out_0.rearrange("(p t) j -> p t j", t=PACK)[:, :, first : first + width], y[u, c][:]
                )

        def planes(u):
            for c, width in PIECES[u]:
                y16 = ring.tile([P, PACK * width], BF16, name="y16", align_bytes=64)
                if u * HALF + c + width == PAIRS:
                    nc.vector.tensor_copy(woven(y16[:], 4), planar(y[u, c][:], 4))
                else:
                    nc.scalar.copy(woven(y16[:], 4), planar(y[u, c][:], 4))
                cols = slice(u * HALF + c, u * HALF + c + width)
                nc.vector.quantize_mx(out=y_codes[:, cols].bitcast(FP8X4), scales=y_scales[:, cols], in_=y16[:])
                nc.sync.dma_start(
                    out_1[0].rearrange("p m t -> p (m t)").bitcast(I32)[:, cols], y_codes[:, cols].bitcast(I32)
                )

        dl_half = difference(1)
        larger(1, 0)
        second_stage(0, quantize(dl_half, "dlq_half0"))
        larger(0, 0)

        for t in range(PACK):
            pick(1, t, 1)
        dl_half = difference(1, shared[:].bitcast(BF16)[:, : PACK * HALF])
        w3q[0] = quantize(w3_parts[0], "w3q0")
        second_stage(1, quantize(dl_half, "dlq_half1"))
        larger(0, 1)
        w3q[1] = quantize(w3_parts[1], "w3q1")
        larger(1, 1)

        third_stage(0)
        third_stage(1)
        planes(0)
        planes(1)
        for q in range(QUADRANTS):
            queue = nc.sync if q % 2 == 0 else nc.scalar
            queue.dma_start(out_2[0, 4 * q : 4 * q + 4, :].bitcast(I32), y_scales[32 * q : 32 * q + 4, :].bitcast(I32))
